import numpy as np
import ml_dtypes


def mxq(x, axis, fmt="e4m3"):
    dtype, down = {"e4m3": (ml_dtypes.float8_e4m3fn, 7), "e5m2": (ml_dtypes.float8_e5m2, 14)}[fmt]
    v = np.moveaxis(np.asarray(x, np.float32).astype(ml_dtypes.bfloat16).astype(np.float64), axis, -1)
    blocks = v.reshape(v.shape[:-1] + (-1, 32))
    amax = np.abs(blocks).max(-1, keepdims=True)
    byte = np.maximum(np.where(amax > 0, np.frexp(amax)[1] - 1 + 127, 0) - down, 1)
    scale = np.exp2(byte - 127.0)
    codes = (blocks / scale).astype(np.float32).astype(dtype).astype(np.float64)
    return np.moveaxis((codes * scale).reshape(v.shape), -1, axis)


WIDE = False


def mx_kscale(k):
    if not WIDE:
        return np.ones(k)
    levels = np.array([10, -10, 5, -5, 0])
    if k % 512:
        return np.exp2(np.random.permutation(np.resize(levels, k // 32))).repeat(32)
    a = np.empty((k // 512, 16))
    for p in range(k // 512):
        a[p, :8] = np.random.permutation(np.resize(levels, 8))
        for g in range(8):
            far = levels[np.abs(levels - a[p, g]) >= 10]
            a[p, g + 8] = far[np.random.randint(len(far))]
    return np.exp2(a.ravel()).repeat(32)


def f64(x):
    return np.asarray(x).astype(np.float64)


def striped(idx):
    return np.tile(np.asarray(idx).reshape(-1, 16).T, (8, 1)).astype(np.uint16)


def unstriped(offs):
    return offs[:16].T.reshape(-1).astype(np.int64)


E2M1 = np.array([0.0, 0.5, 1.0, 1.5, 2.0, 3.0, 4.0, 6.0, -0.0, -0.5, -1.0, -1.5, -2.0, -3.0, -4.0, -6.0])


def pack_weight(w, fmt):
    k, n = w.shape
    w = f64(np.asarray(w, np.float32).astype(ml_dtypes.bfloat16)).reshape(k // 32, 32, n)
    amax = np.abs(w).max(1)
    if fmt == "e4m3":
        byte = np.frexp(amax)[1] - 1 + 127 - 7
    else:
        mant, ex = np.frexp(amax / 6.0)
        byte = np.where(mant > 0.5, ex, ex - 1) + 127
    byte = np.clip(np.where(amax > 0, byte, 1), 1, 254)
    scaled = (w * np.exp2(127.0 - byte)[:, None, :]).reshape(k, n).astype(np.float32)
    by_word = np.ascontiguousarray(scaled.reshape(k // 512, 128, 4, n).transpose(0, 1, 3, 2))
    if fmt == "e4m3":
        words = by_word.astype(ml_dtypes.float8_e4m3fn).view(np.uint8)
    else:
        c = by_word.astype(ml_dtypes.float4_e2m1fn).view(np.uint8) & 0xF
        words = (c[..., 0::2] | (c[..., 1::2] << 4)).reshape(k // 512, 128, 2 * n)
    return np.ascontiguousarray(words), np.ascontiguousarray(byte.astype(np.uint8).reshape(k // 512, 16, n))


def unpack_weight(words, scales, fmt):
    g, _, n = scales.shape
    words = np.ascontiguousarray(words).reshape(g, 128, n, -1)
    if fmt == "e4m3":
        vals = words.view(ml_dtypes.float8_e4m3fn).astype(np.float64)
    else:
        nib = np.empty((g, 128, n, 4), np.uint8)
        nib[..., 0::2] = words & 0xF
        nib[..., 1::2] = words >> 4
        vals = E2M1[nib]
    vals = vals * np.repeat(np.exp2(scales.astype(np.float64) - 127.0), 8, axis=1)[..., None]
    return vals.transpose(0, 1, 3, 2).reshape(g * 512, n)


B, N, T, D, DV, NQ = 1, 512, 2048, 512, 128, 128


def setup_inputs():
    n = np.random.standard_normal
    idx = np.sort(np.random.permutation(T)[:B * N].reshape(B, N), axis=1).reshape(-1)
    s = mx_kscale(D)[:, None]
    u = np.ones(T)
    u[idx] = mx_kscale(B * N)
    r = np.random.uniform(0.5, 2.0, T)
    qp = [pack_weight(x, "e4m3") for x in n((B, D, NQ)) * s * (0.80 / np.sqrt(D))]
    k = n((D, T)) / s
    v = n((DV, T)) / (u * r)
    kp = pack_weight(k, "e4m3")
    return {
        "q_words": np.stack([x[0] for x in qp]),
        "q_scales": np.stack([x[1] for x in qp]),
        "k_words": kp[0],
        "k_scales": kp[1],
        "vT": v.astype(np.float32),
        "vs": np.tile(u * r, (128, 1)).astype(np.float32),
        "kb": np.tile(n(T), (128, 1)).astype(np.float32),
        "og": n((B, NQ, DV)).astype(np.float32),
        "offs": striped(idx),
    }


def reference(q_words, q_scales, k_words, k_scales, vT, vs, kb, og, offs):
    idx = unstriped(offs)
    k = unpack_weight(k_words, k_scales, "e4m3")
    v = f64(vT)
    pick = lambda x: x[:, idx].reshape(x.shape[0], B, N).transpose(1, 0, 2)
    q = np.stack([unpack_weight(q_words[b], q_scales[b], "e4m3") for b in range(B)])
    score = q.transpose(0, 2, 1) @ pick(k)
    score = score + pick(f64(kb))[:, :1, :]
    p = 1.0 / (1.0 + np.exp(-score))
    w = p * pick(f64(vs))[:, :1, :]
    y = mxq(w, 2, "e4m3") @ mxq(pick(v).transpose(0, 2, 1), 1, "e4m3")
    y = y / 16.0
    y = y / (1.0 + np.exp(-f64(og)))
    return y

@@ -1,0 +1,155 @@
+from contextlib import ExitStack
+
+import concourse.mybir as mybir
+from concourse.masks import make_identity
+
+P = 128
+TOKENS = 2048
+SLOTS = 512
+PACK = 4
+BLOCKS = SLOTS // 32
+FLOPS = 2 * 128 * 512 * 512 + 2 * 128 * 512 * 128
+BYTES = 128 * 128 * 4 + 16 * 128 + 128 * 2048 * 4 + 16 * 2048 + 128 * 2048 * 4 + 2 * 2048 * 4 + 2 * 128 * 128 * 4 + 128 * 32 * 2
+
+F32 = mybir.dt.float32
+BF16 = mybir.dt.bfloat16
+I32 = mybir.dt.int32
+U32 = mybir.dt.uint32
+U16 = mybir.dt.uint16
+U8 = mybir.dt.uint8
+FP8X4 = mybir.dt.float8_e4m3fn_x4
+MULT = mybir.AluOpType.mult
+SIGMOID = mybir.ActivationFunctionType.Sigmoid
+
+
+def dealt(ap):
+    return ap.rearrange("p (t b r) -> p b t r", t=PACK, b=BLOCKS)
+
+
+def tile_attend_sigm_kb_gate_srtq128n512t2048_kernel(
+    tc, q_words, q_scales, k_words, k_scales, vT, vs, kb, og, offs, out
+):
+    nc = tc.nc
+    with ExitStack() as ctx:
+        sb = ctx.enter_context(tc.tile_pool(name="sb", bufs=1))
+        ps = ctx.enter_context(tc.psum_pool(name="ps", bufs=1))
+
+        offsets = sb.tile([P, SLOTS // 16], U16, name="offsets")
+        nc.sync.dma_start(offsets[:], offs)
+
+        q_plane = sb.tile([P, P], U8, name="q_plane", align_bytes=64)
+        q_rows = q_scales[0, 0].bitcast(I32)
+        for quad in range(4):
+            nc.sync.dma_start(
+                q_plane[32 * quad : 32 * quad + 32, :].bitcast(I32),
+                q_rows[4 * quad : 4 * quad + 4, :].unsqueeze(0).to_broadcast([8, 4, 32]),
+            )
+
+        k_pool = sb.tile([P, TOKENS], I32, name="k_pool")
+        nc.sync.dma_start(k_pool[:], k_words[0].rearrange("p n t -> p (n t)").bitcast(I32))
+        v_pool = sb.tile([P, TOKENS], F32, name="v_pool")
+        nc.sync.dma_start(v_pool[:], vT)
+
+        gate_in = sb.tile([P, P], F32, name="gate_in")
+        nc.gpsimd.dma_start(gate_in[:], og[0])
+        q_codes = sb.tile([P, P], I32, name="q_codes", align_bytes=64)
+        nc.gpsimd.dma_start(q_codes[:], q_words[0, 0].rearrange("p n t -> p (n t)").bitcast(I32))
+
+        kb_pool = sb.tile([P, TOKENS], F32, name="kb_pool", tag="kb_then_k_codes", align_bytes=64)
+        nc.vector.memset(kb_pool[:].bitcast(I32), 0)
+        nc.scalar.dma_start(kb_pool[0:1, :], kb[0:1, :])
+
+        ks_pool = sb.tile([P, TOKENS], U8, name="ks_pool")
+        nc.vector.memset(ks_pool[:].bitcast(I32), 0)
+        ks_rows = k_scales[0].bitcast(I32)
+        for quad in range(4):
+            nc.scalar.dma_start(
+                ks_pool[32 * quad : 32 * quad + 4, :].bitcast(I32),
+                ks_rows[4 * quad : 4 * quad + 4, :],
+            )
+
+        vs_pool = sb.tile([P, TOKENS], F32, name="vs_pool")
+        nc.vector.memset(vs_pool[:].bitcast(I32), 0)
+        nc.scalar.dma_start(vs_pool[0:1, :], vs[0:1, :])
+
+        ident_f32 = sb.tile([P, P], F32, name="ident_f32")
+        make_identity(nc, ident_f32[:])
+
+        gate = sb.tile([P, P], F32, name="gate")
+        nc.scalar.activation(gate[:], gate_in[:], SIGMOID)
+
+        kb_slots = sb.tile([P, SLOTS], F32, name="kb_slots")
+        nc.vector.tensor_copy(dealt(kb_slots[:].bitcast(U32)), kb_pool[:].bitcast(U32).indirect(offsets[:]))
+        kb_turned = ps.tile([P, PACK, P], F32, name="kb_turned")
+        for t in range(PACK):
+            nc.tensor.transpose(kb_turned[:, t, :], kb_slots[:, t * P : (t + 1) * P], ident_f32[:])
+        kb_col = sb.tile([P, PACK], F32, name="kb_col")
+        nc.scalar.copy(kb_col[:], kb_turned[:, :, 0])
+
+        ks_slots = sb.tile([P, SLOTS], U8, name="ks_slots", tag="ks_then_v")
+        nc.vector.tensor_copy(ks_slots[:], ks_pool[:].indirect(offsets[:]))
+        k_plane = sb.tile([P, SLOTS], U8, name="k_plane", align_bytes=64)
+        nc.vector.tensor_copy(
+            k_plane[:].bitcast(I32).rearrange("p (t b w) -> p t b w", t=PACK, b=BLOCKS),
+            ks_slots[:].bitcast(I32).rearrange("p (b t w) -> p t b w", t=PACK, b=BLOCKS),
+        )
+
+        k_codes = sb.tile([P, SLOTS], U32, name="k_codes", tag="kb_then_k_codes", align_bytes=64)
+        nc.vector.tensor_copy(dealt(k_codes[:]), k_pool[:].bitcast(U32).indirect(offsets[:]))
+
+        p = sb.tile([P, PACK, P], F32, name="p")
+        for t in range(PACK):
+            cols = slice(t * P, (t + 1) * P)
+            scores = ps.tile([P, P], F32, name="scores%d" % t)
+            nc.tensor.matmul_mx(
+                out=scores[:],
+                lhsT=k_codes[:, cols].bitcast(FP8X4),
+                lhsT_scale=k_plane[:, cols],
+                rhs=q_codes[:].bitcast(FP8X4),
+                rhs_scale=q_plane[:],
+                start=True,
+                stop=True,
+            )
+            nc.scalar.activation(p[:, t, :], scores[:], SIGMOID, bias=kb_col[:, t : t + 1])
+
+        vs_slots = sb.tile([P, SLOTS], F32, name="vs_slots")
+        nc.vector.tensor_copy(dealt(vs_slots[:].bitcast(U32)), vs_pool[:].bitcast(U32).indirect(offsets[:]))
+        vs_turned = ps.tile([P, PACK, P], F32, name="vs_turned")
+        for t in range(PACK):
+            nc.tensor.transpose(vs_turned[:, t, :], vs_slots[:, t * P : (t + 1) * P], ident_f32[:])
+
+        v_slots = sb.tile([P, SLOTS], F32, name="v_slots", tag="ks_then_v")
+        nc.vector.tensor_copy(dealt(v_slots[:].bitcast(U32)), v_pool[:].bitcast(U32).indirect(offsets[:]))
+        v_turned = ps.tile([P, PACK, P], F32, name="v_turned")
+        for t in range(PACK):
+            nc.tensor.transpose(v_turned[:, t, :], v_slots[:, t * P : (t + 1) * P], ident_f32[:])
+        v_words = sb.tile([P, P, PACK], BF16, name="v_words", align_bytes=64)
+        nc.scalar.copy(v_words[:], v_turned[:].rearrange("p t e -> p e t"))
+
+        w_words = sb.tile([P, P, PACK], BF16, name="w_words", align_bytes=64)
+        nc.vector.tensor_tensor(
+            w_words[:],
+            p[:].rearrange("p t q -> p q t"),
+            vs_turned[:, :, 0:1].rearrange("p t one -> p one t").to_broadcast([P, P, PACK]),
+            MULT,
+        )
+        w_codes = sb.tile([P, P], U32, name="w_codes", align_bytes=64)
+        w_plane = sb.tile([P, P], U8, name="w_plane", align_bytes=64)
+        nc.vector.quantize_mx(w_codes[:].bitcast(FP8X4), w_plane[:], w_words[:].rearrange("p q t -> p (q t)"))
+        v_codes = sb.tile([P, P], U32, name="v_codes", align_bytes=64)
+        v_plane = sb.tile([P, P], U8, name="v_plane", align_bytes=64)
+        nc.vector.quantize_mx(v_codes[:].bitcast(FP8X4), v_plane[:], v_words[:].rearrange("p e t -> p (e t)"))
+
+        y = ps.tile([P, P], F32, name="y")
+        nc.tensor.matmul_mx(
+            out=y[:],
+            lhsT=w_codes[:].bitcast(FP8X4),
+            lhsT_scale=w_plane[:],
+            rhs=v_codes[:].bitcast(FP8X4),
+            rhs_scale=v_plane[:],
+            start=True,
+            stop=True,
+        )
+        result = sb.tile([P, P], F32, name="result")
+        nc.vector.scalar_tensor_tensor(result[:], y[:], 1.0 / 16.0, gate[:], MULT, MULT)
+        nc.sync.dma_start(out[0], result[:])

@@ -7,7 +7,6 @@ P = 128
 TOKENS = 2048
 SLOTS = 512
 PACK = 4
-BLOCKS = SLOTS // 32
 FLOPS = 2 * 128 * 512 * 512 + 2 * 128 * 512 * 128
 BYTES = 128 * 128 * 4 + 16 * 128 + 128 * 2048 * 4 + 16 * 2048 + 128 * 2048 * 4 + 2 * 2048 * 4 + 2 * 128 * 128 * 4 + 128 * 32 * 2
 
@@ -22,80 +21,79 @@ MULT = mybir.AluOpType.mult
 SIGMOID = mybir.ActivationFunctionType.Sigmoid
 
 
-def dealt(ap):
-    return ap.rearrange("p (t b r) -> p b t r", t=PACK, b=BLOCKS)
-
-
 def tile_attend_sigm_kb_gate_srtq128n512t2048_kernel(
     tc, q_words, q_scales, k_words, k_scales, vT, vs, kb, og, offs, out
 ):
     nc = tc.nc
     with ExitStack() as ctx:
         sb = ctx.enter_context(tc.tile_pool(name="sb", bufs=1))
+        reuse = ctx.enter_context(tc.tile_pool(name="reuse", bufs=1))
         ps = ctx.enter_context(tc.psum_pool(name="ps", bufs=1))
 
         offsets = sb.tile([P, SLOTS // 16], U16, name="offsets")
         nc.sync.dma_start(offsets[:], offs)
-
-        q_plane = sb.tile([P, P], U8, name="q_plane", align_bytes=64)
-        q_rows = q_scales[0, 0].bitcast(I32)
-        for quad in range(4):
-            nc.sync.dma_start(
-                q_plane[32 * quad : 32 * quad + 32, :].bitcast(I32),
-                q_rows[4 * quad : 4 * quad + 4, :].unsqueeze(0).to_broadcast([8, 4, 32]),
-            )
-
-        k_pool = sb.tile([P, TOKENS], I32, name="k_pool")
-        nc.sync.dma_start(k_pool[:], k_words[0].rearrange("p n t -> p (n t)").bitcast(I32))
-        v_pool = sb.tile([P, TOKENS], F32, name="v_pool")
-        nc.sync.dma_start(v_pool[:], vT)
-
         gate_in = sb.tile([P, P], F32, name="gate_in")
-        nc.gpsimd.dma_start(gate_in[:], og[0])
-        q_codes = sb.tile([P, P], I32, name="q_codes", align_bytes=64)
-        nc.gpsimd.dma_start(q_codes[:], q_words[0, 0].rearrange("p n t -> p (n t)").bitcast(I32))
-
-        kb_pool = sb.tile([P, TOKENS], F32, name="kb_pool", tag="kb_then_k_codes", align_bytes=64)
-        nc.vector.memset(kb_pool[:].bitcast(I32), 0)
-        nc.scalar.dma_start(kb_pool[0:1, :], kb[0:1, :])
+        nc.sync.dma_start(gate_in[:], og[0])
 
         ks_pool = sb.tile([P, TOKENS], U8, name="ks_pool")
         nc.vector.memset(ks_pool[:].bitcast(I32), 0)
         ks_rows = k_scales[0].bitcast(I32)
         for quad in range(4):
-            nc.scalar.dma_start(
-                ks_pool[32 * quad : 32 * quad + 4, :].bitcast(I32),
-                ks_rows[4 * quad : 4 * quad + 4, :],
+            nc.sync.dma_start(
+                ks_pool[32 * quad : 32 * quad + 4, :].bitcast(I32), ks_rows[4 * quad : 4 * quad + 4, :]
+            )
+
+        kb_pool = reuse.tile([P, TOKENS], F32, name="kb_pool", offset=0, align_bytes=64)
+        nc.vector.memset(kb_pool[:].bitcast(I32), 0)
+        nc.sync.dma_start(kb_pool[0:1, :], kb[0:1, :])
+
+        k_pool = sb.tile([P, TOKENS], I32, name="k_pool")
+        nc.sync.dma_start(k_pool[:], k_words[0].rearrange("p n t -> p (n t)").bitcast(I32))
+        q_codes = sb.tile([P, P], I32, name="q_codes", align_bytes=64)
+        nc.sync.dma_start(q_codes[:], q_words[0, 0].rearrange("p n t -> p (n t)").bitcast(I32))
+
+        q_plane = sb.tile([P, P], U8, name="q_plane", align_bytes=64)
+        nc.vector.memset(q_plane[:].bitcast(I32), 0)
+        q_rows = q_scales[0, 0].bitcast(I32)
+        for quad in range(4):
+            nc.sync.dma_start(
+                q_plane[32 * quad : 32 * quad + 4, :].bitcast(I32), q_rows[4 * quad : 4 * quad + 4, :]
             )
 
         vs_pool = sb.tile([P, TOKENS], F32, name="vs_pool")
         nc.vector.memset(vs_pool[:].bitcast(I32), 0)
-        nc.scalar.dma_start(vs_pool[0:1, :], vs[0:1, :])
+        nc.sync.dma_start(vs_pool[0:1, :], vs[0:1, :])
 
-        ident_f32 = sb.tile([P, P], F32, name="ident_f32")
-        make_identity(nc, ident_f32[:])
+        v_pool = sb.tile([P, TOKENS], F32, name="v_pool", tag="v_pool_then_w_words", align_bytes=64)
+        nc.sync.dma_start(v_pool[:], vT)
 
         gate = sb.tile([P, P], F32, name="gate")
         nc.scalar.activation(gate[:], gate_in[:], SIGMOID)
+        ident = sb.tile([P, P], F32, name="ident")
+        nc.vector.memset(ident[:], 0.0)
+        make_identity(nc, ident[:], nomemset=True)
+
+        ks_slots = sb.tile([P, SLOTS], U8, name="ks_slots")
+        nc.vector.tensor_copy(ks_slots[:], ks_pool[:].indirect(offsets[:]))
 
         kb_slots = sb.tile([P, SLOTS], F32, name="kb_slots")
-        nc.vector.tensor_copy(dealt(kb_slots[:].bitcast(U32)), kb_pool[:].bitcast(U32).indirect(offsets[:]))
+        nc.vector.tensor_copy(kb_slots[:], kb_pool[:].indirect(offsets[:]))
+        k_plane = reuse.tile([P, SLOTS], U8, name="k_plane", offset=4 * SLOTS, align_bytes=64)
+        nc.vector.tensor_copy(
+            k_plane[:].rearrange("p (t m) -> p t m", t=PACK),
+            ks_slots[:].rearrange("p (m t) -> p t m", t=PACK),
+        )
+
         kb_turned = ps.tile([P, PACK, P], F32, name="kb_turned")
         for t in range(PACK):
-            nc.tensor.transpose(kb_turned[:, t, :], kb_slots[:, t * P : (t + 1) * P], ident_f32[:])
+            nc.tensor.transpose(kb_turned[:, t, :], kb_slots[:, t::PACK], ident[:])
         kb_col = sb.tile([P, PACK], F32, name="kb_col")
         nc.scalar.copy(kb_col[:], kb_turned[:, :, 0])
 
-        ks_slots = sb.tile([P, SLOTS], U8, name="ks_slots", tag="ks_then_v")
-        nc.vector.tensor_copy(ks_slots[:], ks_pool[:].indirect(offsets[:]))
-        k_plane = sb.tile([P, SLOTS], U8, name="k_plane", align_bytes=64)
+        k_codes = reuse.tile([P, SLOTS], U32, name="k_codes", offset=0, align_bytes=64)
         nc.vector.tensor_copy(
-            k_plane[:].bitcast(I32).rearrange("p (t b w) -> p t b w", t=PACK, b=BLOCKS),
-            ks_slots[:].bitcast(I32).rearrange("p (b t w) -> p t b w", t=PACK, b=BLOCKS),
+            k_codes[:].rearrange("p (t m) -> p m t", t=PACK), k_pool[:].bitcast(U32).indirect(offsets[:])
         )
-
-        k_codes = sb.tile([P, SLOTS], U32, name="k_codes", tag="kb_then_k_codes", align_bytes=64)
-        nc.vector.tensor_copy(dealt(k_codes[:]), k_pool[:].bitcast(U32).indirect(offsets[:]))
 
         p = sb.tile([P, PACK, P], F32, name="p")
         for t in range(PACK):
@@ -113,20 +111,21 @@ def tile_attend_sigm_kb_gate_srtq128n512t2048_kernel(
             nc.scalar.activation(p[:, t, :], scores[:], SIGMOID, bias=kb_col[:, t : t + 1])
 
         vs_slots = sb.tile([P, SLOTS], F32, name="vs_slots")
-        nc.vector.tensor_copy(dealt(vs_slots[:].bitcast(U32)), vs_pool[:].bitcast(U32).indirect(offsets[:]))
+        nc.vector.tensor_copy(vs_slots[:], vs_pool[:].indirect(offsets[:]))
         vs_turned = ps.tile([P, PACK, P], F32, name="vs_turned")
         for t in range(PACK):
-            nc.tensor.transpose(vs_turned[:, t, :], vs_slots[:, t * P : (t + 1) * P], ident_f32[:])
+            nc.tensor.transpose(vs_turned[:, t, :], vs_slots[:, t::PACK], ident[:])
 
-        v_slots = sb.tile([P, SLOTS], F32, name="v_slots", tag="ks_then_v")
-        nc.vector.tensor_copy(dealt(v_slots[:].bitcast(U32)), v_pool[:].bitcast(U32).indirect(offsets[:]))
-        v_turned = ps.tile([P, PACK, P], F32, name="v_turned")
-        for t in range(PACK):
-            nc.tensor.transpose(v_turned[:, t, :], v_slots[:, t * P : (t + 1) * P], ident_f32[:])
+        v_slots = sb.tile([P, SLOTS], BF16, name="v_slots")
+        nc.vector.tensor_copy(v_slots[:], v_pool[:].indirect(offsets[:]))
+        v_pairs = v_slots[:].bitcast(F32)
+        v_turned = ps.tile([P, 2, P], F32, name="v_turned")
+        for u in range(2):
+            nc.tensor.transpose(v_turned[:, u, :], v_pairs[:, u::2], ident[:])
         v_words = sb.tile([P, P, PACK], BF16, name="v_words", align_bytes=64)
-        nc.scalar.copy(v_words[:], v_turned[:].rearrange("p t e -> p e t"))
+        nc.scalar.copy(v_words[:].bitcast(F32), v_turned[:].rearrange("p u e -> p e u"))
 
-        w_words = sb.tile([P, P, PACK], BF16, name="w_words", align_bytes=64)
+        w_words = sb.tile([P, P, PACK], BF16, name="w_words", tag="v_pool_then_w_words", align_bytes=64)
         nc.vector.tensor_tensor(
             w_words[:],
             p[:].rearrange("p t q -> p q t"),

@@ -111,10 +111,13 @@ def tile_attend_sigm_kb_gate_srtq128n512t2048_kernel(
             nc.scalar.activation(p[:, t, :], scores[:], SIGMOID, bias=kb_col[:, t : t + 1])
 
         vs_slots = sb.tile([P, SLOTS], F32, name="vs_slots")
-        nc.vector.tensor_copy(vs_slots[:], vs_pool[:].indirect(offsets[:]))
+        nc.vector.tensor_copy(
+            vs_slots[:].bitcast(U32).rearrange("p (t m) -> p m t", t=PACK),
+            vs_pool[:].bitcast(U32).indirect(offsets[:]),
+        )
         vs_turned = ps.tile([P, PACK, P], F32, name="vs_turned")
         for t in range(PACK):
-            nc.tensor.transpose(vs_turned[:, t, :], vs_slots[:, t::PACK], ident[:])
+            nc.tensor.transpose(vs_turned[:, t, :], vs_slots[:, t * P : (t + 1) * P], ident[:])
 
         v_slots = sb.tile([P, SLOTS], BF16, name="v_slots")
         nc.vector.tensor_copy(v_slots[:], v_pool[:].indirect(offsets[:]))

@@ -7,6 +7,7 @@ P = 128
 TOKENS = 2048
 SLOTS = 512
 PACK = 4
+ROW = P - 1
 FLOPS = 2 * 128 * 512 * 512 + 2 * 128 * 512 * 128
 BYTES = 128 * 128 * 4 + 16 * 128 + 128 * 2048 * 4 + 16 * 2048 + 128 * 2048 * 4 + 2 * 2048 * 4 + 2 * 128 * 128 * 4 + 128 * 32 * 2
 
@@ -32,20 +33,21 @@ def tile_attend_sigm_kb_gate_srtq128n512t2048_kernel(
 
         offsets = sb.tile([P, SLOTS // 16], U16, name="offsets")
         nc.sync.dma_start(offsets[:], offs)
-        gate_in = sb.tile([P, P], F32, name="gate_in")
-        nc.sync.dma_start(gate_in[:], og[0])
 
         ks_pool = sb.tile([P, TOKENS], U8, name="ks_pool")
         nc.vector.memset(ks_pool[:].bitcast(I32), 0)
+        kb_pool = reuse.tile([P, TOKENS], F32, name="kb_pool", offset=0, align_bytes=64)
+        nc.sync.dma_start(kb_pool[ROW : ROW + 1, :], kb[0:1, :])
+        nc.vector.memset(kb_pool[0:ROW, :].bitcast(I32), 0)
+
+        gate_in = sb.tile([P, P], F32, name="gate_in")
+        nc.sync.dma_start(gate_in[:], og[0])
+
         ks_rows = k_scales[0].bitcast(I32)
         for quad in range(4):
             nc.sync.dma_start(
                 ks_pool[32 * quad : 32 * quad + 4, :].bitcast(I32), ks_rows[4 * quad : 4 * quad + 4, :]
             )
-
-        kb_pool = reuse.tile([P, TOKENS], F32, name="kb_pool", offset=0, align_bytes=64)
-        nc.vector.memset(kb_pool[:].bitcast(I32), 0)
-        nc.sync.dma_start(kb_pool[0:1, :], kb[0:1, :])
 
         k_pool = sb.tile([P, TOKENS], I32, name="k_pool")
         nc.sync.dma_start(k_pool[:], k_words[0].rearrange("p n t -> p (n t)").bitcast(I32))
@@ -61,8 +63,8 @@ def tile_attend_sigm_kb_gate_srtq128n512t2048_kernel(
             )
 
         vs_pool = sb.tile([P, TOKENS], F32, name="vs_pool")
-        nc.vector.memset(vs_pool[:].bitcast(I32), 0)
-        nc.sync.dma_start(vs_pool[0:1, :], vs[0:1, :])
+        nc.sync.dma_start(vs_pool[ROW : ROW + 1, :], vs[0:1, :])
+        nc.vector.memset(vs_pool[0:ROW, :].bitcast(I32), 0)
 
         v_pool = sb.tile([P, TOKENS], F32, name="v_pool", tag="v_pool_then_w_words", align_bytes=64)
         nc.sync.dma_start(v_pool[:], vT)
@@ -70,8 +72,7 @@ def tile_attend_sigm_kb_gate_srtq128n512t2048_kernel(
         gate = sb.tile([P, P], F32, name="gate")
         nc.scalar.activation(gate[:], gate_in[:], SIGMOID)
         ident = sb.tile([P, P], F32, name="ident")
-        nc.vector.memset(ident[:], 0.0)
-        make_identity(nc, ident[:], nomemset=True)
+        make_identity(nc, ident[:])
 
         ks_slots = sb.tile([P, SLOTS], U8, name="ks_slots")
         nc.vector.tensor_copy(ks_slots[:], ks_pool[:].indirect(offsets[:]))
@@ -88,7 +89,7 @@ def tile_attend_sigm_kb_gate_srtq128n512t2048_kernel(
         for t in range(PACK):
             nc.tensor.transpose(kb_turned[:, t, :], kb_slots[:, t::PACK], ident[:])
         kb_col = sb.tile([P, PACK], F32, name="kb_col")
-        nc.scalar.copy(kb_col[:], kb_turned[:, :, 0])
+        nc.scalar.copy(kb_col[:], kb_turned[:, :, ROW])
 
         k_codes = reuse.tile([P, SLOTS], U32, name="k_codes", offset=0, align_bytes=64)
         nc.vector.tensor_copy(
@@ -132,7 +133,7 @@ def tile_attend_sigm_kb_gate_srtq128n512t2048_kernel(
         nc.vector.tensor_tensor(
             w_words[:],
             p[:].rearrange("p t q -> p q t"),
-            vs_turned[:, :, 0:1].rearrange("p t one -> p one t").to_broadcast([P, P, PACK]),
+            vs_turned[:, :, ROW : ROW + 1].rearrange("p t one -> p one t").to_broadcast([P, P, PACK]),
             MULT,
         )
         w_codes = sb.tile([P, P], U32, name="w_codes", align_bytes=64)

@@ -7,6 +7,7 @@ P = 128
 TOKENS = 2048
 SLOTS = 512
 PACK = 4
+HEAD = 64
 ROW = P - 1
 FLOPS = 2 * 128 * 512 * 512 + 2 * 128 * 512 * 128
 BYTES = 128 * 128 * 4 + 16 * 128 + 128 * 2048 * 4 + 16 * 2048 + 128 * 2048 * 4 + 2 * 2048 * 4 + 2 * 128 * 128 * 4 + 128 * 32 * 2
@@ -64,15 +65,17 @@ def tile_attend_sigm_kb_gate_srtq128n512t2048_kernel(
 
         vs_pool = sb.tile([P, TOKENS], F32, name="vs_pool")
         nc.sync.dma_start(vs_pool[ROW : ROW + 1, :], vs[0:1, :])
-        nc.vector.memset(vs_pool[0:ROW, :].bitcast(I32), 0)
+        ident = sb.tile([P, P], F32, name="ident")
+        nc.vector.memset(ident[:], 0.0)
+        make_identity(nc, ident[:], nomemset=True)
+        nc.vector.memset(vs_pool[0:ROW, 0:HEAD].bitcast(I32), 0)
+        nc.gpsimd.memset(vs_pool[0:ROW, HEAD - 8 :].bitcast(I32), 0)
 
         v_pool = sb.tile([P, TOKENS], F32, name="v_pool", tag="v_pool_then_w_words", align_bytes=64)
         nc.sync.dma_start(v_pool[:], vT)
 
         gate = sb.tile([P, P], F32, name="gate")
         nc.scalar.activation(gate[:], gate_in[:], SIGMOID)
-        ident = sb.tile([P, P], F32, name="ident")
-        make_identity(nc, ident[:])
 
         ks_slots = sb.tile([P, SLOTS], U8, name="ks_slots")
         nc.vector.tensor_copy(ks_slots[:], ks_pool[:].indirect(offsets[:]))

@@ -35,14 +35,14 @@ def tile_attend_sigm_kb_gate_srtq128n512t2048_kernel(
         offsets = sb.tile([P, SLOTS // 16], U16, name="offsets")
         nc.sync.dma_start(offsets[:], offs)
 
-        ks_pool = sb.tile([P, TOKENS], U8, name="ks_pool")
+        ks_pool = sb.tile([P, TOKENS], U8, name="ks_pool", tag="ks_pool_then_kb_col")
         nc.vector.memset(ks_pool[:].bitcast(I32), 0)
         kb_pool = reuse.tile([P, TOKENS], F32, name="kb_pool", offset=0, align_bytes=64)
         nc.sync.dma_start(kb_pool[ROW : ROW + 1, :], kb[0:1, :])
         nc.vector.memset(kb_pool[0:ROW, :].bitcast(I32), 0)
 
-        gate_in = sb.tile([P, P], F32, name="gate_in")
-        nc.sync.dma_start(gate_in[:], og[0])
+        vs_pool = sb.tile([P, TOKENS], F32, name="vs_pool")
+        nc.sync.dma_start(vs_pool[ROW : ROW + 1, :], vs[0:1, :])
 
         ks_rows = k_scales[0].bitcast(I32)
         for quad in range(4):
@@ -63,8 +63,6 @@ def tile_attend_sigm_kb_gate_srtq128n512t2048_kernel(
                 q_plane[32 * quad : 32 * quad + 4, :].bitcast(I32), q_rows[4 * quad : 4 * quad + 4, :]
             )
 
-        vs_pool = sb.tile([P, TOKENS], F32, name="vs_pool")
-        nc.sync.dma_start(vs_pool[ROW : ROW + 1, :], vs[0:1, :])
         ident = sb.tile([P, P], F32, name="ident")
         nc.vector.memset(ident[:], 0.0)
         make_identity(nc, ident[:], nomemset=True)
@@ -73,9 +71,9 @@ def tile_attend_sigm_kb_gate_srtq128n512t2048_kernel(
 
         v_pool = sb.tile([P, TOKENS], F32, name="v_pool", tag="v_pool_then_w_words", align_bytes=64)
         nc.sync.dma_start(v_pool[:], vT)
+        gate_in = sb.tile([P, P], F32, name="gate_in")
+        nc.sync.dma_start(gate_in[:], og[0])
 
-        gate = sb.tile([P, P], F32, name="gate")
-        nc.scalar.activation(gate[:], gate_in[:], SIGMOID)
 
         ks_slots = sb.tile([P, SLOTS], U8, name="ks_slots")
         nc.vector.tensor_copy(ks_slots[:], ks_pool[:].indirect(offsets[:]))
@@ -91,8 +89,8 @@ def tile_attend_sigm_kb_gate_srtq128n512t2048_kernel(
         kb_turned = ps.tile([P, PACK, P], F32, name="kb_turned")
         for t in range(PACK):
             nc.tensor.transpose(kb_turned[:, t, :], kb_slots[:, t::PACK], ident[:])
-        kb_col = sb.tile([P, PACK], F32, name="kb_col")
-        nc.scalar.copy(kb_col[:], kb_turned[:, :, ROW])
+        kb_col = sb.tile([P, PACK], F32, name="kb_col", tag="ks_pool_then_kb_col")
+        nc.vector.tensor_copy(kb_col[:], kb_turned[:, :, ROW])
 
         k_codes = reuse.tile([P, SLOTS], U32, name="k_codes", offset=0, align_bytes=64)
         nc.vector.tensor_copy(
@@ -113,6 +111,9 @@ def tile_attend_sigm_kb_gate_srtq128n512t2048_kernel(
                 stop=True,
             )
             nc.scalar.activation(p[:, t, :], scores[:], SIGMOID, bias=kb_col[:, t : t + 1])
+
+        gate = sb.tile([P, P], F32, name="gate")
+        nc.scalar.activation(gate[:], gate_in[:], SIGMOID)
 
         vs_slots = sb.tile([P, SLOTS], F32, name="vs_slots")
         nc.vector.tensor_copy(

@@ -45,10 +45,8 @@ def tile_attend_sigm_kb_gate_srtq128n512t2048_kernel(
         nc.sync.dma_start(vs_pool[ROW : ROW + 1, :], vs[0:1, :])
 
         ks_rows = k_scales[0].bitcast(I32)
-        for quad in range(4):
-            nc.sync.dma_start(
-                ks_pool[32 * quad : 32 * quad + 4, :].bitcast(I32), ks_rows[4 * quad : 4 * quad + 4, :]
-            )
+        for r in range(4):
+            nc.sync.dma_start(ks_pool[r:P:32, :].bitcast(I32), ks_rows[r:16:4, :])
 
         k_pool = sb.tile([P, TOKENS], I32, name="k_pool")
         nc.sync.dma_start(k_pool[:], k_words[0].rearrange("p n t -> p (n t)").bitcast(I32))
@@ -58,10 +56,8 @@ def tile_attend_sigm_kb_gate_srtq128n512t2048_kernel(
         q_plane = sb.tile([P, P], U8, name="q_plane", align_bytes=64)
         nc.vector.memset(q_plane[:].bitcast(I32), 0)
         q_rows = q_scales[0, 0].bitcast(I32)
-        for quad in range(4):
-            nc.sync.dma_start(
-                q_plane[32 * quad : 32 * quad + 4, :].bitcast(I32), q_rows[4 * quad : 4 * quad + 4, :]
-            )
+        for r in range(4):
+            nc.sync.dma_start(q_plane[r:P:32, :].bitcast(I32), q_rows[r:16:4, :])
 
         ident = sb.tile([P, P], F32, name="ident")
         nc.vector.memset(ident[:], 0.0)

@@ -7,7 +7,7 @@ P = 128
 TOKENS = 2048
 SLOTS = 512
 PACK = 4
-HEAD = 64
+HEAD = 256
 ROW = P - 1
 FLOPS = 2 * 128 * 512 * 512 + 2 * 128 * 512 * 128
 BYTES = 128 * 128 * 4 + 16 * 128 + 128 * 2048 * 4 + 16 * 2048 + 128 * 2048 * 4 + 2 * 2048 * 4 + 2 * 128 * 128 * 4 + 128 * 32 * 2
@@ -71,22 +71,28 @@ def tile_attend_sigm_kb_gate_srtq128n512t2048_kernel(
         nc.sync.dma_start(gate_in[:], og[0])
 
 
+        kb_slots = sb.tile([P, SLOTS], F32, name="kb_slots")
+        nc.vector.tensor_copy(kb_slots[:], kb_pool[:].indirect(offsets[:]))
+        kb_turned = ps.tile([P, PACK, P], F32, name="kb_turned")
+        for t in range(PACK):
+            nc.tensor.transpose(kb_turned[:, t, :], kb_slots[:, t::PACK], ident[:])
+
         ks_slots = sb.tile([P, SLOTS], U8, name="ks_slots")
         nc.vector.tensor_copy(ks_slots[:], ks_pool[:].indirect(offsets[:]))
 
-        kb_slots = sb.tile([P, SLOTS], F32, name="kb_slots")
-        nc.vector.tensor_copy(kb_slots[:], kb_pool[:].indirect(offsets[:]))
+        vs_slots = sb.tile([P, SLOTS], F32, name="vs_slots")
+        nc.vector.tensor_copy(vs_slots[:], vs_pool[:].indirect(offsets[:]))
+        vs_turned = ps.tile([P, PACK, P], F32, name="vs_turned")
+        for t in range(PACK):
+            nc.tensor.transpose(vs_turned[:, t, :], vs_slots[:, t::PACK], ident[:])
+
+        kb_col = sb.tile([P, PACK], F32, name="kb_col", tag="ks_pool_then_kb_col")
+        nc.vector.tensor_copy(kb_col[:], kb_turned[:, :, ROW])
         k_plane = reuse.tile([P, SLOTS], U8, name="k_plane", offset=4 * SLOTS, align_bytes=64)
         nc.vector.tensor_copy(
             k_plane[:].rearrange("p (t m) -> p t m", t=PACK),
             ks_slots[:].rearrange("p (m t) -> p t m", t=PACK),
         )
-
-        kb_turned = ps.tile([P, PACK, P], F32, name="kb_turned")
-        for t in range(PACK):
-            nc.tensor.transpose(kb_turned[:, t, :], kb_slots[:, t::PACK], ident[:])
-        kb_col = sb.tile([P, PACK], F32, name="kb_col", tag="ks_pool_then_kb_col")
-        nc.vector.tensor_copy(kb_col[:], kb_turned[:, :, ROW])
 
         k_codes = reuse.tile([P, SLOTS], U32, name="k_codes", offset=0, align_bytes=64)
         nc.vector.tensor_copy(
@@ -110,15 +116,6 @@ def tile_attend_sigm_kb_gate_srtq128n512t2048_kernel(
 
         gate = sb.tile([P, P], F32, name="gate")
         nc.scalar.activation(gate[:], gate_in[:], SIGMOID)
-
-        vs_slots = sb.tile([P, SLOTS], F32, name="vs_slots")
-        nc.vector.tensor_copy(
-            vs_slots[:].bitcast(U32).rearrange("p (t m) -> p m t", t=PACK),
-            vs_pool[:].bitcast(U32).indirect(offsets[:]),
-        )
-        vs_turned = ps.tile([P, PACK, P], F32, name="vs_turned")
-        for t in range(PACK):
-            nc.tensor.transpose(vs_turned[:, t, :], vs_slots[:, t * P : (t + 1) * P], ident[:])
 
         v_slots = sb.tile([P, SLOTS], BF16, name="v_slots")
         nc.vector.tensor_copy(v_slots[:], v_pool[:].indirect(offsets[:]))

@@ -7,6 +7,8 @@ P = 128
 TOKENS = 2048
 SLOTS = 512
 PACK = 4
+RUN = 4
+LINE = 4
 HEAD = 256
 ROW = P - 1
 FLOPS = 2 * 128 * 512 * 512 + 2 * 128 * 512 * 128
@@ -23,22 +25,25 @@ MULT = mybir.AluOpType.mult
 SIGMOID = mybir.ActivationFunctionType.Sigmoid
 
 
+def dealt(words):
+    return words.rearrange("p (t c i) -> p c t i", t=PACK, i=RUN)
+
+
 def tile_attend_sigm_kb_gate_srtq128n512t2048_kernel(
     tc, q_words, q_scales, k_words, k_scales, vT, vs, kb, og, offs, out
 ):
     nc = tc.nc
     with ExitStack() as ctx:
         sb = ctx.enter_context(tc.tile_pool(name="sb", bufs=1))
-        reuse = ctx.enter_context(tc.tile_pool(name="reuse", bufs=1))
         ps = ctx.enter_context(tc.psum_pool(name="ps", bufs=1))
 
+        kb_pool = sb.tile([P, TOKENS], F32, name="kb_pool")
+        nc.sync.dma_start(kb_pool[ROW : ROW + 1, :], kb[0:1, :])
         offsets = sb.tile([P, SLOTS // 16], U16, name="offsets")
         nc.sync.dma_start(offsets[:], offs)
 
         ks_pool = sb.tile([P, TOKENS], U8, name="ks_pool", tag="ks_pool_then_kb_col")
         nc.vector.memset(ks_pool[:].bitcast(I32), 0)
-        kb_pool = reuse.tile([P, TOKENS], F32, name="kb_pool", offset=0, align_bytes=64)
-        nc.sync.dma_start(kb_pool[ROW : ROW + 1, :], kb[0:1, :])
         nc.vector.memset(kb_pool[0:ROW, :].bitcast(I32), 0)
 
         vs_pool = sb.tile([P, TOKENS], F32, name="vs_pool")
@@ -70,34 +75,31 @@ def tile_attend_sigm_kb_gate_srtq128n512t2048_kernel(
         gate_in = sb.tile([P, P], F32, name="gate_in")
         nc.sync.dma_start(gate_in[:], og[0])
 
-
         kb_slots = sb.tile([P, SLOTS], F32, name="kb_slots")
-        nc.vector.tensor_copy(kb_slots[:], kb_pool[:].indirect(offsets[:]))
+        nc.vector.tensor_copy(dealt(kb_slots[:].bitcast(U32)), kb_pool[:].bitcast(U32).indirect(offsets[:]))
         kb_turned = ps.tile([P, PACK, P], F32, name="kb_turned")
         for t in range(PACK):
-            nc.tensor.transpose(kb_turned[:, t, :], kb_slots[:, t::PACK], ident[:])
+            nc.tensor.transpose(kb_turned[:, t, :], kb_slots[:, t * P : (t + 1) * P], ident[:])
 
         ks_slots = sb.tile([P, SLOTS], U8, name="ks_slots")
         nc.vector.tensor_copy(ks_slots[:], ks_pool[:].indirect(offsets[:]))
 
         vs_slots = sb.tile([P, SLOTS], F32, name="vs_slots")
-        nc.vector.tensor_copy(vs_slots[:], vs_pool[:].indirect(offsets[:]))
+        nc.vector.tensor_copy(dealt(vs_slots[:].bitcast(U32)), vs_pool[:].bitcast(U32).indirect(offsets[:]))
         vs_turned = ps.tile([P, PACK, P], F32, name="vs_turned")
         for t in range(PACK):
-            nc.tensor.transpose(vs_turned[:, t, :], vs_slots[:, t::PACK], ident[:])
+            nc.tensor.transpose(vs_turned[:, t, :], vs_slots[:, t * P : (t + 1) * P], ident[:])
 
         kb_col = sb.tile([P, PACK], F32, name="kb_col", tag="ks_pool_then_kb_col")
         nc.vector.tensor_copy(kb_col[:], kb_turned[:, :, ROW])
-        k_plane = reuse.tile([P, SLOTS], U8, name="k_plane", offset=4 * SLOTS, align_bytes=64)
+        k_plane = sb.tile([P, SLOTS], U8, name="k_plane", align_bytes=64)
         nc.vector.tensor_copy(
-            k_plane[:].rearrange("p (t m) -> p t m", t=PACK),
-            ks_slots[:].rearrange("p (m t) -> p t m", t=PACK),
+            k_plane[:].bitcast(I32).rearrange("p (t c) -> p t c", t=PACK),
+            ks_slots[:].bitcast(I32).rearrange("p (c t) -> p t c", t=PACK),
         )
 
-        k_codes = reuse.tile([P, SLOTS], U32, name="k_codes", offset=0, align_bytes=64)
-        nc.vector.tensor_copy(
-            k_codes[:].rearrange("p (t m) -> p m t", t=PACK), k_pool[:].bitcast(U32).indirect(offsets[:])
-        )
+        k_codes = sb.tile([P, SLOTS], U32, name="k_codes", align_bytes=64)
+        nc.vector.tensor_copy(dealt(k_codes[:]), k_pool[:].bitcast(U32).indirect(offsets[:]))
 
         p = sb.tile([P, PACK, P], F32, name="p")
         for t in range(PACK):
@@ -118,19 +120,21 @@ def tile_attend_sigm_kb_gate_srtq128n512t2048_kernel(
         nc.scalar.activation(gate[:], gate_in[:], SIGMOID)
 
         v_slots = sb.tile([P, SLOTS], BF16, name="v_slots")
-        nc.vector.tensor_copy(v_slots[:], v_pool[:].indirect(offsets[:]))
+        nc.vector.tensor_copy(
+            v_slots[:].rearrange("p (u c i j) -> p c u j i", u=2, i=RUN, j=2), v_pool[:].indirect(offsets[:])
+        )
         v_pairs = v_slots[:].bitcast(F32)
         v_turned = ps.tile([P, 2, P], F32, name="v_turned")
         for u in range(2):
-            nc.tensor.transpose(v_turned[:, u, :], v_pairs[:, u::2], ident[:])
+            nc.tensor.transpose(v_turned[:, u, :], v_pairs[:, u * P : (u + 1) * P], ident[:])
         v_words = sb.tile([P, P, PACK], BF16, name="v_words", align_bytes=64)
         nc.scalar.copy(v_words[:].bitcast(F32), v_turned[:].rearrange("p u e -> p e u"))
 
         w_words = sb.tile([P, P, PACK], BF16, name="w_words", tag="v_pool_then_w_words", align_bytes=64)
         nc.vector.tensor_tensor(
-            w_words[:],
-            p[:].rearrange("p t q -> p q t"),
-            vs_turned[:, :, ROW : ROW + 1].rearrange("p t one -> p one t").to_broadcast([P, P, PACK]),
+            w_words[:].rearrange("p (c i) t -> p c t i", i=LINE),
+            p[:].rearrange("p t (c i) -> p c t i", i=LINE),
+            vs_turned[:, :, ROW : ROW + 1].unsqueeze(1).to_broadcast([P, P // LINE, PACK, LINE]),
             MULT,
         )
         w_codes = sb.tile([P, P], U32, name="w_codes", align_bytes=64)

@@ -61,8 +61,6 @@ def tile_attend_sigm_kb_gate_srtq128n512t2048_kernel(
         q_plane = sb.tile([P, P], U8, name="q_plane", align_bytes=64)
         nc.vector.memset(q_plane[:].bitcast(I32), 0)
         q_rows = q_scales[0, 0].bitcast(I32)
-        for r in range(4):
-            nc.sync.dma_start(q_plane[r:P:32, :].bitcast(I32), q_rows[r:16:4, :])
 
         ident = sb.tile([P, P], F32, name="ident")
         nc.vector.memset(ident[:], 0.0)
@@ -72,6 +70,8 @@ def tile_attend_sigm_kb_gate_srtq128n512t2048_kernel(
 
         v_pool = sb.tile([P, TOKENS], F32, name="v_pool", tag="v_pool_then_w_words", align_bytes=64)
         nc.sync.dma_start(v_pool[:], vT)
+        for r in range(4):
+            nc.sync.dma_start(q_plane[r:P:32, :].bitcast(I32), q_rows[r:16:4, :])
         gate_in = sb.tile([P, P], F32, name="gate_in")
         nc.sync.dma_start(gate_in[:], og[0])
 
@@ -124,7 +124,7 @@ def tile_attend_sigm_kb_gate_srtq128n512t2048_kernel(
             v_slots[:].rearrange("p (u c i j) -> p c u j i", u=2, i=RUN, j=2), v_pool[:].indirect(offsets[:])
         )
         v_pairs = v_slots[:].bitcast(F32)
-        v_turned = ps.tile([P, 2, P], F32, name="v_turned")
+        v_turned = ps.tile([P, 2, P], F32, name="v_turned", tag="scores0")
         for u in range(2):
             nc.tensor.transpose(v_turned[:, u, :], v_pairs[:, u * P : (u + 1) * P], ident[:])
         v_words = sb.tile([P, P, PACK], BF16, name="v_words", align_bytes=64)

@@ -9,7 +9,7 @@ SLOTS = 512
 PACK = 4
 RUN = 4
 LINE = 4
-HEAD = 256
+HEAD = 64
 ROW = P - 1
 FLOPS = 2 * 128 * 512 * 512 + 2 * 128 * 512 * 128
 BYTES = 128 * 128 * 4 + 16 * 128 + 128 * 2048 * 4 + 16 * 2048 + 128 * 2048 * 4 + 2 * 2048 * 4 + 2 * 128 * 128 * 4 + 128 * 32 * 2
@@ -37,43 +37,33 @@ def tile_attend_sigm_kb_gate_srtq128n512t2048_kernel(
         sb = ctx.enter_context(tc.tile_pool(name="sb", bufs=1))
         ps = ctx.enter_context(tc.psum_pool(name="ps", bufs=1))
 
-        kb_pool = sb.tile([P, TOKENS], F32, name="kb_pool")
-        nc.sync.dma_start(kb_pool[ROW : ROW + 1, :], kb[0:1, :])
         offsets = sb.tile([P, SLOTS // 16], U16, name="offsets")
-        nc.sync.dma_start(offsets[:], offs)
-
         ks_pool = sb.tile([P, TOKENS], U8, name="ks_pool", tag="ks_pool_then_kb_col")
-        nc.vector.memset(ks_pool[:].bitcast(I32), 0)
-        nc.vector.memset(kb_pool[0:ROW, :].bitcast(I32), 0)
-
+        kb_pool = sb.tile([P, TOKENS], F32, name="kb_pool")
         vs_pool = sb.tile([P, TOKENS], F32, name="vs_pool")
-        nc.sync.dma_start(vs_pool[ROW : ROW + 1, :], vs[0:1, :])
-
-        ks_rows = k_scales[0].bitcast(I32)
-        for r in range(4):
-            nc.sync.dma_start(ks_pool[r:P:32, :].bitcast(I32), ks_rows[r:16:4, :])
-
+        staged = sb.tile([P, SLOTS + P], U8, name="staged")
+        planes = sb.tile([P, SLOTS + P], U8, name="planes", align_bytes=64)
         k_pool = sb.tile([P, TOKENS], I32, name="k_pool")
-        nc.sync.dma_start(k_pool[:], k_words[0].rearrange("p n t -> p (n t)").bitcast(I32))
         q_codes = sb.tile([P, P], I32, name="q_codes", align_bytes=64)
-        nc.sync.dma_start(q_codes[:], q_words[0, 0].rearrange("p n t -> p (n t)").bitcast(I32))
-
-        q_plane = sb.tile([P, P], U8, name="q_plane", align_bytes=64)
-        nc.vector.memset(q_plane[:].bitcast(I32), 0)
-        q_rows = q_scales[0, 0].bitcast(I32)
-
+        v_pool = sb.tile([P, TOKENS], F32, name="v_pool", tag="v_pool_then_w_words", align_bytes=64)
         ident = sb.tile([P, P], F32, name="ident")
+
+        nc.vector.memset(ks_pool[:].bitcast(I32), 0)
+        nc.sync.dma_start(kb_pool[ROW : ROW + 1, :], kb[0:1, :])
+        nc.sync.dma_start(offsets[:], offs)
+        nc.sync.dma_start(vs_pool[ROW : ROW + 1, :], vs[0:1, :])
+        nc.sync.dma_start(ks_pool[0:P:8, :].bitcast(I32), k_scales[0].bitcast(I32))
+        nc.sync.dma_start(staged[0:P:8, SLOTS:].bitcast(I32), q_scales[0, 0].bitcast(I32))
+        nc.sync.dma_start(k_pool[:], k_words[0].rearrange("p n t -> p (n t)").bitcast(I32))
+        nc.sync.dma_start(q_codes[:], q_words[0, 0].rearrange("p n t -> p (n t)").bitcast(I32))
+        nc.sync.dma_start(v_pool[:], vT)
+
+        nc.vector.memset(kb_pool[0:ROW, :].bitcast(I32), 0)
+        nc.vector.memset(planes[:].bitcast(I32), 0)
         nc.vector.memset(ident[:], 0.0)
         make_identity(nc, ident[:], nomemset=True)
         nc.vector.memset(vs_pool[0:ROW, 0:HEAD].bitcast(I32), 0)
         nc.gpsimd.memset(vs_pool[0:ROW, HEAD - 8 :].bitcast(I32), 0)
-
-        v_pool = sb.tile([P, TOKENS], F32, name="v_pool", tag="v_pool_then_w_words", align_bytes=64)
-        nc.sync.dma_start(v_pool[:], vT)
-        for r in range(4):
-            nc.sync.dma_start(q_plane[r:P:32, :].bitcast(I32), q_rows[r:16:4, :])
-        gate_in = sb.tile([P, P], F32, name="gate_in")
-        nc.sync.dma_start(gate_in[:], og[0])
 
         kb_slots = sb.tile([P, SLOTS], F32, name="kb_slots")
         nc.vector.tensor_copy(dealt(kb_slots[:].bitcast(U32)), kb_pool[:].bitcast(U32).indirect(offsets[:]))
@@ -81,8 +71,21 @@ def tile_attend_sigm_kb_gate_srtq128n512t2048_kernel(
         for t in range(PACK):
             nc.tensor.transpose(kb_turned[:, t, :], kb_slots[:, t * P : (t + 1) * P], ident[:])
 
-        ks_slots = sb.tile([P, SLOTS], U8, name="ks_slots")
+        ks_slots = sb.tile([P, SLOTS], U8, name="ks_slots", tag="ks_slots_then_gate_in")
         nc.vector.tensor_copy(ks_slots[:], ks_pool[:].indirect(offsets[:]))
+        kb_col = sb.tile([P, PACK], F32, name="kb_col", tag="ks_pool_then_kb_col")
+        nc.vector.tensor_copy(kb_col[:], kb_turned[:, :, ROW])
+        nc.vector.tensor_copy(
+            staged[:, 0:SLOTS].bitcast(I32).rearrange("p (t c) -> p t c", t=PACK),
+            ks_slots[:].bitcast(I32).rearrange("p (c t) -> p t c", t=PACK),
+        )
+        for r in range(4):
+            nc.sync.dma_start(planes[r:P:32, :].bitcast(I32), staged[8 * r : P : 32, :].bitcast(I32))
+        gate_in = sb.tile([P, P], F32, name="gate_in", tag="ks_slots_then_gate_in")
+        nc.sync.dma_start(gate_in[:], og[0])
+
+        k_codes = sb.tile([P, SLOTS], U32, name="k_codes", align_bytes=64)
+        nc.vector.tensor_copy(dealt(k_codes[:]), k_pool[:].bitcast(U32).indirect(offsets[:]))
 
         vs_slots = sb.tile([P, SLOTS], F32, name="vs_slots")
         nc.vector.tensor_copy(dealt(vs_slots[:].bitcast(U32)), vs_pool[:].bitcast(U32).indirect(offsets[:]))
@@ -90,27 +93,16 @@ def tile_attend_sigm_kb_gate_srtq128n512t2048_kernel(
         for t in range(PACK):
             nc.tensor.transpose(vs_turned[:, t, :], vs_slots[:, t * P : (t + 1) * P], ident[:])
 
-        kb_col = sb.tile([P, PACK], F32, name="kb_col", tag="ks_pool_then_kb_col")
-        nc.vector.tensor_copy(kb_col[:], kb_turned[:, :, ROW])
-        k_plane = sb.tile([P, SLOTS], U8, name="k_plane", align_bytes=64)
-        nc.vector.tensor_copy(
-            k_plane[:].bitcast(I32).rearrange("p (t c) -> p t c", t=PACK),
-            ks_slots[:].bitcast(I32).rearrange("p (c t) -> p t c", t=PACK),
-        )
-
-        k_codes = sb.tile([P, SLOTS], U32, name="k_codes", align_bytes=64)
-        nc.vector.tensor_copy(dealt(k_codes[:]), k_pool[:].bitcast(U32).indirect(offsets[:]))
-
-        p = sb.tile([P, PACK, P], F32, name="p")
+        p = sb.tile([P, PACK, P], F32, name="p", tag="p_then_v_codes", align_bytes=64)
         for t in range(PACK):
             cols = slice(t * P, (t + 1) * P)
             scores = ps.tile([P, P], F32, name="scores%d" % t)
             nc.tensor.matmul_mx(
                 out=scores[:],
                 lhsT=k_codes[:, cols].bitcast(FP8X4),
-                lhsT_scale=k_plane[:, cols],
+                lhsT_scale=planes[:, cols],
                 rhs=q_codes[:].bitcast(FP8X4),
-                rhs_scale=q_plane[:],
+                rhs_scale=planes[:, SLOTS:],
                 start=True,
                 stop=True,
             )
@@ -140,7 +132,7 @@ def tile_attend_sigm_kb_gate_srtq128n512t2048_kernel(
         w_codes = sb.tile([P, P], U32, name="w_codes", align_bytes=64)
         w_plane = sb.tile([P, P], U8, name="w_plane", align_bytes=64)
         nc.vector.quantize_mx(w_codes[:].bitcast(FP8X4), w_plane[:], w_words[:].rearrange("p q t -> p (q t)"))
-        v_codes = sb.tile([P, P], U32, name="v_codes", align_bytes=64)
+        v_codes = sb.tile([P, P], U32, name="v_codes", tag="p_then_v_codes", align_bytes=64)
         v_plane = sb.tile([P, P], U8, name="v_plane", align_bytes=64)
         nc.vector.quantize_mx(v_codes[:].bitcast(FP8X4), v_plane[:], v_words[:].rearrange("p e t -> p (e t)"))
 

@@ -9,8 +9,9 @@ SLOTS = 512
 PACK = 4
 RUN = 4
 LINE = 4
-HEAD = 64
+HEAD = 1216
 ROW = P - 1
+STAGE = P - 16
 FLOPS = 2 * 128 * 512 * 512 + 2 * 128 * 512 * 128
 BYTES = 128 * 128 * 4 + 16 * 128 + 128 * 2048 * 4 + 16 * 2048 + 128 * 2048 * 4 + 2 * 2048 * 4 + 2 * 128 * 128 * 4 + 128 * 32 * 2
 
@@ -38,9 +39,9 @@ def tile_attend_sigm_kb_gate_srtq128n512t2048_kernel(
         ps = ctx.enter_context(tc.psum_pool(name="ps", bufs=1))
 
         offsets = sb.tile([P, SLOTS // 16], U16, name="offsets")
-        ks_pool = sb.tile([P, TOKENS], U8, name="ks_pool", tag="ks_pool_then_kb_col")
+        ks_pool = sb.tile([P, TOKENS], U8, name="ks_pool")
         kb_pool = sb.tile([P, TOKENS], F32, name="kb_pool")
-        vs_pool = sb.tile([P, TOKENS], F32, name="vs_pool")
+        vs_pool = sb.tile([P, TOKENS], F32, name="vs_pool", tag="vs_pool_then_kb_col")
         staged = sb.tile([P, SLOTS + P], U8, name="staged")
         planes = sb.tile([P, SLOTS + P], U8, name="planes", align_bytes=64)
         k_pool = sb.tile([P, TOKENS], I32, name="k_pool")
@@ -48,16 +49,16 @@ def tile_attend_sigm_kb_gate_srtq128n512t2048_kernel(
         v_pool = sb.tile([P, TOKENS], F32, name="v_pool", tag="v_pool_then_w_words", align_bytes=64)
         ident = sb.tile([P, P], F32, name="ident")
 
-        nc.vector.memset(ks_pool[:].bitcast(I32), 0)
+        nc.sync.dma_start(ks_pool[STAGE:P, :].bitcast(I32), k_scales[0].bitcast(I32))
         nc.sync.dma_start(kb_pool[ROW : ROW + 1, :], kb[0:1, :])
         nc.sync.dma_start(offsets[:], offs)
         nc.sync.dma_start(vs_pool[ROW : ROW + 1, :], vs[0:1, :])
-        nc.sync.dma_start(ks_pool[0:P:8, :].bitcast(I32), k_scales[0].bitcast(I32))
-        nc.sync.dma_start(staged[0:P:8, SLOTS:].bitcast(I32), q_scales[0, 0].bitcast(I32))
         nc.sync.dma_start(k_pool[:], k_words[0].rearrange("p n t -> p (n t)").bitcast(I32))
+        nc.sync.dma_start(staged[STAGE:P, SLOTS:].bitcast(I32), q_scales[0, 0].bitcast(I32))
         nc.sync.dma_start(q_codes[:], q_words[0, 0].rearrange("p n t -> p (n t)").bitcast(I32))
         nc.sync.dma_start(v_pool[:], vT)
 
+        nc.vector.memset(ks_pool[0:STAGE, :].bitcast(I32), 0)
         nc.vector.memset(kb_pool[0:ROW, :].bitcast(I32), 0)
         nc.vector.memset(planes[:].bitcast(I32), 0)
         nc.vector.memset(ident[:], 0.0)
@@ -65,27 +66,23 @@ def tile_attend_sigm_kb_gate_srtq128n512t2048_kernel(
         nc.vector.memset(vs_pool[0:ROW, 0:HEAD].bitcast(I32), 0)
         nc.gpsimd.memset(vs_pool[0:ROW, HEAD - 8 :].bitcast(I32), 0)
 
+        ks_slots = sb.tile([P, SLOTS], U8, name="ks_slots", tag="ks_slots_then_gate_in")
+        nc.vector.tensor_copy(ks_slots[:], ks_pool[:].indirect(offsets[:]))
+
         kb_slots = sb.tile([P, SLOTS], F32, name="kb_slots")
         nc.vector.tensor_copy(dealt(kb_slots[:].bitcast(U32)), kb_pool[:].bitcast(U32).indirect(offsets[:]))
-        kb_turned = ps.tile([P, PACK, P], F32, name="kb_turned")
+        kb_turned = ps.tile([P, PACK, P], F32, name="kb_turned", tag="first_bank")
         for t in range(PACK):
             nc.tensor.transpose(kb_turned[:, t, :], kb_slots[:, t * P : (t + 1) * P], ident[:])
 
-        ks_slots = sb.tile([P, SLOTS], U8, name="ks_slots", tag="ks_slots_then_gate_in")
-        nc.vector.tensor_copy(ks_slots[:], ks_pool[:].indirect(offsets[:]))
-        kb_col = sb.tile([P, PACK], F32, name="kb_col", tag="ks_pool_then_kb_col")
-        nc.vector.tensor_copy(kb_col[:], kb_turned[:, :, ROW])
         nc.vector.tensor_copy(
             staged[:, 0:SLOTS].bitcast(I32).rearrange("p (t c) -> p t c", t=PACK),
             ks_slots[:].bitcast(I32).rearrange("p (c t) -> p t c", t=PACK),
         )
         for r in range(4):
-            nc.sync.dma_start(planes[r:P:32, :].bitcast(I32), staged[8 * r : P : 32, :].bitcast(I32))
+            nc.sync.dma_start(planes[r:P:32, :].bitcast(I32), staged[STAGE + r : P : 4, :].bitcast(I32))
         gate_in = sb.tile([P, P], F32, name="gate_in", tag="ks_slots_then_gate_in")
         nc.sync.dma_start(gate_in[:], og[0])
-
-        k_codes = sb.tile([P, SLOTS], U32, name="k_codes", align_bytes=64)
-        nc.vector.tensor_copy(dealt(k_codes[:]), k_pool[:].bitcast(U32).indirect(offsets[:]))
 
         vs_slots = sb.tile([P, SLOTS], F32, name="vs_slots")
         nc.vector.tensor_copy(dealt(vs_slots[:].bitcast(U32)), vs_pool[:].bitcast(U32).indirect(offsets[:]))
@@ -93,10 +90,16 @@ def tile_attend_sigm_kb_gate_srtq128n512t2048_kernel(
         for t in range(PACK):
             nc.tensor.transpose(vs_turned[:, t, :], vs_slots[:, t * P : (t + 1) * P], ident[:])
 
+        k_codes = sb.tile([P, SLOTS], U32, name="k_codes", align_bytes=64)
+        nc.vector.tensor_copy(dealt(k_codes[:]), k_pool[:].bitcast(U32).indirect(offsets[:]))
+
+        kb_col = sb.tile([P, PACK], F32, name="kb_col", tag="vs_pool_then_kb_col")
+        nc.vector.tensor_copy(kb_col[:], kb_turned[:, :, ROW])
+
         p = sb.tile([P, PACK, P], F32, name="p", tag="p_then_v_codes", align_bytes=64)
         for t in range(PACK):
             cols = slice(t * P, (t + 1) * P)
-            scores = ps.tile([P, P], F32, name="scores%d" % t)
+            scores = ps.tile([P, P], F32, name="scores%d" % t, tag="scores%d" % t if t else "first_bank")
             nc.tensor.matmul_mx(
                 out=scores[:],
                 lhsT=k_codes[:, cols].bitcast(FP8X4),
@@ -116,7 +119,7 @@ def tile_attend_sigm_kb_gate_srtq128n512t2048_kernel(
             v_slots[:].rearrange("p (u c i j) -> p c u j i", u=2, i=RUN, j=2), v_pool[:].indirect(offsets[:])
         )
         v_pairs = v_slots[:].bitcast(F32)
-        v_turned = ps.tile([P, 2, P], F32, name="v_turned", tag="scores0")
+        v_turned = ps.tile([P, 2, P], F32, name="v_turned", tag="first_bank")
         for u in range(2):
             nc.tensor.transpose(v_turned[:, u, :], v_pairs[:, u * P : (u + 1) * P], ident[:])
         v_words = sb.tile([P, P, PACK], BF16, name="v_words", align_bytes=64)

@@ -9,7 +9,7 @@ SLOTS = 512
 PACK = 4
 RUN = 4
 LINE = 4
-HEAD = 1216
+HEAD = 640
 ROW = P - 1
 STAGE = P - 16
 FLOPS = 2 * 128 * 512 * 512 + 2 * 128 * 512 * 128
@@ -61,9 +61,9 @@ def tile_attend_sigm_kb_gate_srtq128n512t2048_kernel(
         nc.vector.memset(ks_pool[0:STAGE, :].bitcast(I32), 0)
         nc.vector.memset(kb_pool[0:ROW, :].bitcast(I32), 0)
         nc.vector.memset(planes[:].bitcast(I32), 0)
+        nc.vector.memset(vs_pool[0:ROW, 0:HEAD].bitcast(I32), 0)
         nc.vector.memset(ident[:], 0.0)
         make_identity(nc, ident[:], nomemset=True)
-        nc.vector.memset(vs_pool[0:ROW, 0:HEAD].bitcast(I32), 0)
         nc.gpsimd.memset(vs_pool[0:ROW, HEAD - 8 :].bitcast(I32), 0)
 
         ks_slots = sb.tile([P, SLOTS], U8, name="ks_slots", tag="ks_slots_then_gate_in")

@@ -41,10 +41,10 @@ def tile_attend_sigm_kb_gate_srtq128n512t2048_kernel(
         offsets = sb.tile([P, SLOTS // 16], U16, name="offsets")
         ks_pool = sb.tile([P, TOKENS], U8, name="ks_pool")
         kb_pool = sb.tile([P, TOKENS], F32, name="kb_pool")
-        vs_pool = sb.tile([P, TOKENS], F32, name="vs_pool", tag="vs_pool_then_kb_col")
+        vs_pool = sb.tile([P, TOKENS], F32, name="vs_pool")
         staged = sb.tile([P, SLOTS + P], U8, name="staged")
         planes = sb.tile([P, SLOTS + P], U8, name="planes", align_bytes=64)
-        k_pool = sb.tile([P, TOKENS], I32, name="k_pool")
+        k_pool = sb.tile([P, TOKENS], I32, name="k_pool", tag="k_pool_then_kb_col")
         q_codes = sb.tile([P, P], I32, name="q_codes", align_bytes=64)
         v_pool = sb.tile([P, TOKENS], F32, name="v_pool", tag="v_pool_then_w_words", align_bytes=64)
         ident = sb.tile([P, P], F32, name="ident")
@@ -55,15 +55,15 @@ def tile_attend_sigm_kb_gate_srtq128n512t2048_kernel(
         nc.sync.dma_start(vs_pool[ROW : ROW + 1, :], vs[0:1, :])
         nc.sync.dma_start(k_pool[:], k_words[0].rearrange("p n t -> p (n t)").bitcast(I32))
         nc.sync.dma_start(staged[STAGE:P, SLOTS:].bitcast(I32), q_scales[0, 0].bitcast(I32))
-        nc.sync.dma_start(q_codes[:], q_words[0, 0].rearrange("p n t -> p (n t)").bitcast(I32))
         nc.sync.dma_start(v_pool[:], vT)
+        nc.sync.dma_start(q_codes[:], q_words[0, 0].rearrange("p n t -> p (n t)").bitcast(I32))
 
         nc.vector.memset(ks_pool[0:STAGE, :].bitcast(I32), 0)
         nc.vector.memset(kb_pool[0:ROW, :].bitcast(I32), 0)
         nc.vector.memset(planes[:].bitcast(I32), 0)
-        nc.vector.memset(vs_pool[0:ROW, 0:HEAD].bitcast(I32), 0)
         nc.vector.memset(ident[:], 0.0)
         make_identity(nc, ident[:], nomemset=True)
+        nc.vector.memset(vs_pool[0:ROW, 0:HEAD].bitcast(I32), 0)
         nc.gpsimd.memset(vs_pool[0:ROW, HEAD - 8 :].bitcast(I32), 0)
 
         ks_slots = sb.tile([P, SLOTS], U8, name="ks_slots", tag="ks_slots_then_gate_in")
@@ -84,17 +84,17 @@ def tile_attend_sigm_kb_gate_srtq128n512t2048_kernel(
         gate_in = sb.tile([P, P], F32, name="gate_in", tag="ks_slots_then_gate_in")
         nc.sync.dma_start(gate_in[:], og[0])
 
+        k_codes = sb.tile([P, SLOTS], U32, name="k_codes", align_bytes=64)
+        nc.vector.tensor_copy(dealt(k_codes[:]), k_pool[:].bitcast(U32).indirect(offsets[:]))
+
+        kb_col = sb.tile([P, PACK], F32, name="kb_col", tag="k_pool_then_kb_col")
+        nc.vector.tensor_copy(kb_col[:], kb_turned[:, :, ROW])
+
         vs_slots = sb.tile([P, SLOTS], F32, name="vs_slots")
         nc.vector.tensor_copy(dealt(vs_slots[:].bitcast(U32)), vs_pool[:].bitcast(U32).indirect(offsets[:]))
         vs_turned = ps.tile([P, PACK, P], F32, name="vs_turned")
         for t in range(PACK):
             nc.tensor.transpose(vs_turned[:, t, :], vs_slots[:, t * P : (t + 1) * P], ident[:])
-
-        k_codes = sb.tile([P, SLOTS], U32, name="k_codes", align_bytes=64)
-        nc.vector.tensor_copy(dealt(k_codes[:]), k_pool[:].bitcast(U32).indirect(offsets[:]))
-
-        kb_col = sb.tile([P, PACK], F32, name="kb_col", tag="vs_pool_then_kb_col")
-        nc.vector.tensor_copy(kb_col[:], kb_turned[:, :, ROW])
 
         p = sb.tile([P, PACK, P], F32, name="p", tag="p_then_v_codes", align_bytes=64)
         for t in range(PACK):

@@ -8,7 +8,6 @@ TOKENS = 2048
 SLOTS = 512
 PACK = 4
 RUN = 4
-LINE = 4
 HEAD = 640
 ROW = P - 1
 STAGE = P - 16
@@ -126,12 +125,8 @@ def tile_attend_sigm_kb_gate_srtq128n512t2048_kernel(
         nc.scalar.copy(v_words[:].bitcast(F32), v_turned[:].rearrange("p u e -> p e u"))
 
         w_words = sb.tile([P, P, PACK], BF16, name="w_words", tag="v_pool_then_w_words", align_bytes=64)
-        nc.vector.tensor_tensor(
-            w_words[:].rearrange("p (c i) t -> p c t i", i=LINE),
-            p[:].rearrange("p t (c i) -> p c t i", i=LINE),
-            vs_turned[:, :, ROW : ROW + 1].unsqueeze(1).to_broadcast([P, P // LINE, PACK, LINE]),
-            MULT,
-        )
+        for t in range(PACK):
+            nc.vector.tensor_scalar_mul(w_words[:, :, t], p[:, t, :], vs_turned[:, t, ROW : ROW + 1])
         w_codes = sb.tile([P, P], U32, name="w_codes", align_bytes=64)
         w_plane = sb.tile([P, P], U8, name="w_plane", align_bytes=64)
         nc.vector.quantize_mx(w_codes[:].bitcast(FP8X4), w_plane[:], w_words[:].rearrange("p q t -> p (q t)"))

@@ -43,9 +43,9 @@ def tile_attend_sigm_kb_gate_srtq128n512t2048_kernel(
         vs_pool = sb.tile([P, TOKENS], F32, name="vs_pool")
         staged = sb.tile([P, SLOTS + P], U8, name="staged")
         planes = sb.tile([P, SLOTS + P], U8, name="planes", align_bytes=64)
-        k_pool = sb.tile([P, TOKENS], I32, name="k_pool", tag="k_pool_then_kb_col")
+        k_pool = sb.tile([P, TOKENS], I32, name="k_pool")
         q_codes = sb.tile([P, P], I32, name="q_codes", align_bytes=64)
-        v_pool = sb.tile([P, TOKENS], F32, name="v_pool", tag="v_pool_then_w_words", align_bytes=64)
+        v_pool = sb.tile([P, TOKENS], F32, name="v_pool")
         ident = sb.tile([P, P], F32, name="ident")
 
         nc.sync.dma_start(ks_pool[STAGE:P, :].bitcast(I32), k_scales[0].bitcast(I32))
@@ -57,6 +57,9 @@ def tile_attend_sigm_kb_gate_srtq128n512t2048_kernel(
         nc.sync.dma_start(v_pool[:], vT)
         nc.sync.dma_start(q_codes[:], q_words[0, 0].rearrange("p n t -> p (n t)").bitcast(I32))
 
+        warm = sb.tile([P, 1], F32, name="warm")
+        nc.gpsimd.memset(warm[:], 0.0)
+        nc.scalar.activation(warm[:], warm[:], SIGMOID)
         nc.vector.memset(ks_pool[0:STAGE, :].bitcast(I32), 0)
         nc.vector.memset(kb_pool[0:ROW, :].bitcast(I32), 0)
         nc.vector.memset(planes[:].bitcast(I32), 0)
@@ -86,8 +89,8 @@ def tile_attend_sigm_kb_gate_srtq128n512t2048_kernel(
         k_codes = sb.tile([P, SLOTS], U32, name="k_codes", align_bytes=64)
         nc.vector.tensor_copy(dealt(k_codes[:]), k_pool[:].bitcast(U32).indirect(offsets[:]))
 
-        kb_col = sb.tile([P, PACK], F32, name="kb_col", tag="k_pool_then_kb_col")
-        nc.vector.tensor_copy(kb_col[:], kb_turned[:, :, ROW])
+        kb_col = sb.tile([P, PACK], F32, name="kb_col")
+        nc.scalar.copy(kb_col[:], kb_turned[:, :, ROW])
 
         vs_slots = sb.tile([P, SLOTS], F32, name="vs_slots")
         nc.vector.tensor_copy(dealt(vs_slots[:].bitcast(U32)), vs_pool[:].bitcast(U32).indirect(offsets[:]))
@@ -124,7 +127,7 @@ def tile_attend_sigm_kb_gate_srtq128n512t2048_kernel(
         v_words = sb.tile([P, P, PACK], BF16, name="v_words", align_bytes=64)
         nc.scalar.copy(v_words[:].bitcast(F32), v_turned[:].rearrange("p u e -> p e u"))
 
-        w_words = sb.tile([P, P, PACK], BF16, name="w_words", tag="v_pool_then_w_words", align_bytes=64)
+        w_words = sb.tile([P, P, PACK], BF16, name="w_words", align_bytes=64)
         for t in range(PACK):
             nc.vector.tensor_scalar_mul(w_words[:, :, t], p[:, t, :], vs_turned[:, t, ROW : ROW + 1])
         w_codes = sb.tile([P, P], U32, name="w_codes", align_bytes=64)

@@ -10,7 +10,7 @@ PACK = 4
 RUN = 4
 HEAD = 640
 ROW = P - 1
-STAGE = P - 16
+STAGE = 48
 FLOPS = 2 * 128 * 512 * 512 + 2 * 128 * 512 * 128
 BYTES = 128 * 128 * 4 + 16 * 128 + 128 * 2048 * 4 + 16 * 2048 + 128 * 2048 * 4 + 2 * 2048 * 4 + 2 * 128 * 128 * 4 + 128 * 32 * 2
 
@@ -23,6 +23,7 @@ U8 = mybir.dt.uint8
 FP8X4 = mybir.dt.float8_e4m3fn_x4
 MULT = mybir.AluOpType.mult
 SIGMOID = mybir.ActivationFunctionType.Sigmoid
+COPY = mybir.ActivationFunctionType.Copy
 
 
 def dealt(words):
@@ -48,12 +49,12 @@ def tile_attend_sigm_kb_gate_srtq128n512t2048_kernel(
         v_pool = sb.tile([P, TOKENS], F32, name="v_pool")
         ident = sb.tile([P, P], F32, name="ident")
 
-        nc.sync.dma_start(ks_pool[STAGE:P, :].bitcast(I32), k_scales[0].bitcast(I32))
         nc.sync.dma_start(kb_pool[ROW : ROW + 1, :], kb[0:1, :])
         nc.sync.dma_start(offsets[:], offs)
         nc.sync.dma_start(vs_pool[ROW : ROW + 1, :], vs[0:1, :])
+        nc.sync.dma_start(ks_pool[STAGE : STAGE + 16, :].bitcast(I32), k_scales[0].bitcast(I32))
         nc.sync.dma_start(k_pool[:], k_words[0].rearrange("p n t -> p (n t)").bitcast(I32))
-        nc.sync.dma_start(staged[STAGE:P, SLOTS:].bitcast(I32), q_scales[0, 0].bitcast(I32))
+        nc.sync.dma_start(staged[STAGE : STAGE + 16, SLOTS:].bitcast(I32), q_scales[0, 0].bitcast(I32))
         nc.sync.dma_start(v_pool[:], vT)
         nc.sync.dma_start(q_codes[:], q_words[0, 0].rearrange("p n t -> p (n t)").bitcast(I32))
 
@@ -61,6 +62,7 @@ def tile_attend_sigm_kb_gate_srtq128n512t2048_kernel(
         nc.gpsimd.memset(warm[:], 0.0)
         nc.scalar.activation(warm[:], warm[:], SIGMOID)
         nc.vector.memset(ks_pool[0:STAGE, :].bitcast(I32), 0)
+        nc.vector.memset(ks_pool[STAGE + 16 :, :].bitcast(I32), 0)
         nc.vector.memset(kb_pool[0:ROW, :].bitcast(I32), 0)
         nc.vector.memset(planes[:].bitcast(I32), 0)
         nc.vector.memset(ident[:], 0.0)
@@ -72,17 +74,22 @@ def tile_attend_sigm_kb_gate_srtq128n512t2048_kernel(
         nc.vector.tensor_copy(ks_slots[:], ks_pool[:].indirect(offsets[:]))
 
         kb_slots = sb.tile([P, SLOTS], F32, name="kb_slots")
-        nc.vector.tensor_copy(dealt(kb_slots[:].bitcast(U32)), kb_pool[:].bitcast(U32).indirect(offsets[:]))
+        nc.scalar.activation(kb_slots[:], kb_pool[:].indirect(offsets[:]), COPY)
+        kb_dealt = sb.tile([P, SLOTS], F32, name="kb_dealt")
+        nc.scalar.copy(
+            kb_dealt[:].rearrange("p (t c i) -> p t c i", t=PACK, i=RUN),
+            kb_slots[:].rearrange("p (c t i) -> p t c i", t=PACK, i=RUN),
+        )
         kb_turned = ps.tile([P, PACK, P], F32, name="kb_turned", tag="first_bank")
         for t in range(PACK):
-            nc.tensor.transpose(kb_turned[:, t, :], kb_slots[:, t * P : (t + 1) * P], ident[:])
+            nc.tensor.transpose(kb_turned[:, t, :], kb_dealt[:, t * P : (t + 1) * P], ident[:])
 
         nc.vector.tensor_copy(
             staged[:, 0:SLOTS].bitcast(I32).rearrange("p (t c) -> p t c", t=PACK),
             ks_slots[:].bitcast(I32).rearrange("p (c t) -> p t c", t=PACK),
         )
         for r in range(4):
-            nc.sync.dma_start(planes[r:P:32, :].bitcast(I32), staged[STAGE + r : P : 4, :].bitcast(I32))
+            nc.sync.dma_start(planes[r:P:32, :].bitcast(I32), staged[STAGE + r : STAGE + 16 : 4, :].bitcast(I32))
         gate_in = sb.tile([P, P], F32, name="gate_in", tag="ks_slots_then_gate_in")
         nc.sync.dma_start(gate_in[:], og[0])
 

@@ -49,6 +49,9 @@ def tile_attend_sigm_kb_gate_srtq128n512t2048_kernel(
         v_pool = sb.tile([P, TOKENS], F32, name="v_pool")
         ident = sb.tile([P, P], F32, name="ident")
 
+        gate_in = sb.tile([P, P], F32, name="gate_in", tag="gate_in_then_kb_slots")
+        nc.scalar.dma_start(gate_in[:], og[0])
+        nc.scalar.dma_start(q_codes[:], q_words[0, 0].rearrange("p n t -> p (n t)").bitcast(I32))
         nc.sync.dma_start(kb_pool[ROW : ROW + 1, :], kb[0:1, :])
         nc.sync.dma_start(offsets[:], offs)
         nc.sync.dma_start(vs_pool[ROW : ROW + 1, :], vs[0:1, :])
@@ -56,11 +59,7 @@ def tile_attend_sigm_kb_gate_srtq128n512t2048_kernel(
         nc.sync.dma_start(k_pool[:], k_words[0].rearrange("p n t -> p (n t)").bitcast(I32))
         nc.sync.dma_start(staged[STAGE : STAGE + 16, SLOTS:].bitcast(I32), q_scales[0, 0].bitcast(I32))
         nc.sync.dma_start(v_pool[:], vT)
-        nc.sync.dma_start(q_codes[:], q_words[0, 0].rearrange("p n t -> p (n t)").bitcast(I32))
 
-        warm = sb.tile([P, 1], F32, name="warm")
-        nc.gpsimd.memset(warm[:], 0.0)
-        nc.scalar.activation(warm[:], warm[:], SIGMOID)
         nc.vector.memset(ks_pool[0:STAGE, :].bitcast(I32), 0)
         nc.vector.memset(ks_pool[STAGE + 16 :, :].bitcast(I32), 0)
         nc.vector.memset(kb_pool[0:ROW, :].bitcast(I32), 0)
@@ -70,10 +69,12 @@ def tile_attend_sigm_kb_gate_srtq128n512t2048_kernel(
         nc.vector.memset(vs_pool[0:ROW, 0:HEAD].bitcast(I32), 0)
         nc.gpsimd.memset(vs_pool[0:ROW, HEAD - 8 :].bitcast(I32), 0)
 
-        ks_slots = sb.tile([P, SLOTS], U8, name="ks_slots", tag="ks_slots_then_gate_in")
+        ks_slots = sb.tile([P, SLOTS], U8, name="ks_slots")
         nc.vector.tensor_copy(ks_slots[:], ks_pool[:].indirect(offsets[:]))
 
-        kb_slots = sb.tile([P, SLOTS], F32, name="kb_slots")
+        gate = sb.tile([P, P], F32, name="gate")
+        nc.scalar.activation(gate[:], gate_in[:], SIGMOID)
+        kb_slots = sb.tile([P, SLOTS], F32, name="kb_slots", tag="gate_in_then_kb_slots")
         nc.scalar.activation(kb_slots[:], kb_pool[:].indirect(offsets[:]), COPY)
         kb_dealt = sb.tile([P, SLOTS], F32, name="kb_dealt")
         nc.scalar.copy(
@@ -90,8 +91,6 @@ def tile_attend_sigm_kb_gate_srtq128n512t2048_kernel(
         )
         for r in range(4):
             nc.sync.dma_start(planes[r:P:32, :].bitcast(I32), staged[STAGE + r : STAGE + 16 : 4, :].bitcast(I32))
-        gate_in = sb.tile([P, P], F32, name="gate_in", tag="ks_slots_then_gate_in")
-        nc.sync.dma_start(gate_in[:], og[0])
 
         k_codes = sb.tile([P, SLOTS], U32, name="k_codes", align_bytes=64)
         nc.vector.tensor_copy(dealt(k_codes[:]), k_pool[:].bitcast(U32).indirect(offsets[:]))
@@ -119,9 +118,6 @@ def tile_attend_sigm_kb_gate_srtq128n512t2048_kernel(
                 stop=True,
             )
             nc.scalar.activation(p[:, t, :], scores[:], SIGMOID, bias=kb_col[:, t : t + 1])
-
-        gate = sb.tile([P, P], F32, name="gate")
-        nc.scalar.activation(gate[:], gate_in[:], SIGMOID)
 
         v_slots = sb.tile([P, SLOTS], BF16, name="v_slots")
         nc.vector.tensor_copy(

@@ -8,9 +8,9 @@ TOKENS = 2048
 SLOTS = 512
 PACK = 4
 RUN = 4
-HEAD = 640
 ROW = P - 1
-STAGE = 48
+STAGE = P - 16
+QW = P // 4
 FLOPS = 2 * 128 * 512 * 512 + 2 * 128 * 512 * 128
 BYTES = 128 * 128 * 4 + 16 * 128 + 128 * 2048 * 4 + 16 * 2048 + 128 * 2048 * 4 + 2 * 2048 * 4 + 2 * 128 * 128 * 4 + 128 * 32 * 2
 
@@ -36,67 +36,88 @@ def tile_attend_sigm_kb_gate_srtq128n512t2048_kernel(
     nc = tc.nc
     with ExitStack() as ctx:
         sb = ctx.enter_context(tc.tile_pool(name="sb", bufs=1))
+        reused = ctx.enter_context(tc.tile_pool(name="reused", bufs=1))
         ps = ctx.enter_context(tc.psum_pool(name="ps", bufs=1))
 
         offsets = sb.tile([P, SLOTS // 16], U16, name="offsets")
-        ks_pool = sb.tile([P, TOKENS], U8, name="ks_pool")
+        ks_pool = reused.tile([P, TOKENS], U8, name="ks_pool", offset=1024)
+        gate_in = reused.tile([P, P], F32, name="gate_in", offset=0)
         kb_pool = sb.tile([P, TOKENS], F32, name="kb_pool")
         vs_pool = sb.tile([P, TOKENS], F32, name="vs_pool")
-        staged = sb.tile([P, SLOTS + P], U8, name="staged")
-        planes = sb.tile([P, SLOTS + P], U8, name="planes", align_bytes=64)
+        qs_rows = sb.tile([4, 4, QW], I32, name="qs_rows")
+        planes = sb.tile([P, SLOTS + 2 * P], U8, name="planes", align_bytes=64)
         k_pool = sb.tile([P, TOKENS], I32, name="k_pool")
         q_codes = sb.tile([P, P], I32, name="q_codes", align_bytes=64)
-        v_pool = sb.tile([P, TOKENS], F32, name="v_pool")
         ident = sb.tile([P, P], F32, name="ident")
 
-        gate_in = sb.tile([P, P], F32, name="gate_in", tag="gate_in_then_kb_slots")
-        nc.scalar.dma_start(gate_in[:], og[0])
-        nc.scalar.dma_start(q_codes[:], q_words[0, 0].rearrange("p n t -> p (n t)").bitcast(I32))
-        nc.sync.dma_start(kb_pool[ROW : ROW + 1, :], kb[0:1, :])
+        nc.scalar.dma_start(ks_pool[STAGE:, :].bitcast(I32), k_scales[0].bitcast(I32))
         nc.sync.dma_start(offsets[:], offs)
-        nc.sync.dma_start(vs_pool[ROW : ROW + 1, :], vs[0:1, :])
-        nc.sync.dma_start(ks_pool[STAGE : STAGE + 16, :].bitcast(I32), k_scales[0].bitcast(I32))
+        nc.scalar.dma_start(gate_in[:], og[0])
+        nc.sync.dma_start(kb_pool[ROW : ROW + 1, :], kb[0:1, :])
+        nc.sync.dma_start(qs_rows[:], q_scales[0, 0].bitcast(I32).rearrange("(a j) n -> j a n", j=4))
+        nc.scalar.dma_start(q_codes[:], q_words[0, 0].rearrange("p n t -> p (n t)").bitcast(I32))
         nc.sync.dma_start(k_pool[:], k_words[0].rearrange("p n t -> p (n t)").bitcast(I32))
-        nc.sync.dma_start(staged[STAGE : STAGE + 16, SLOTS:].bitcast(I32), q_scales[0, 0].bitcast(I32))
-        nc.sync.dma_start(v_pool[:], vT)
+        nc.sync.dma_start(vs_pool[ROW : ROW + 1, :], vs[0:1, :])
 
+        plane_words = planes[:].bitcast(I32)
         nc.vector.memset(ks_pool[0:STAGE, :].bitcast(I32), 0)
-        nc.vector.memset(ks_pool[STAGE + 16 :, :].bitcast(I32), 0)
+        nc.vector.memset(plane_words, 0)
         nc.vector.memset(kb_pool[0:ROW, :].bitcast(I32), 0)
-        nc.vector.memset(planes[:].bitcast(I32), 0)
         nc.vector.memset(ident[:], 0.0)
         make_identity(nc, ident[:], nomemset=True)
-        nc.vector.memset(vs_pool[0:ROW, 0:HEAD].bitcast(I32), 0)
-        nc.gpsimd.memset(vs_pool[0:ROW, HEAD - 8 :].bitcast(I32), 0)
 
         ks_slots = sb.tile([P, SLOTS], U8, name="ks_slots")
-        nc.vector.tensor_copy(ks_slots[:], ks_pool[:].indirect(offsets[:]))
+        nc.vector.tensor_copy(dealt(ks_slots[:]), ks_pool[:].indirect(offsets[:]))
 
         gate = sb.tile([P, P], F32, name="gate")
         nc.scalar.activation(gate[:], gate_in[:], SIGMOID)
-        kb_slots = sb.tile([P, SLOTS], F32, name="kb_slots", tag="gate_in_then_kb_slots")
+
+        for r in range(4):
+            queue = nc.sync if r % 2 == 0 else nc.scalar
+            queue.dma_start(plane_words[r:P:32, 0 : SLOTS // 4], ks_slots[STAGE + r : P : 4, :].bitcast(I32))
+        v_pool = reused.tile([P, TOKENS], F32, name="v_pool", offset=2048)
+        nc.sync.dma_start(v_pool[:], vT)
+
+        kb_slots = reused.tile([P, SLOTS], F32, name="kb_slots", offset=0)
         nc.scalar.activation(kb_slots[:], kb_pool[:].indirect(offsets[:]), COPY)
         kb_dealt = sb.tile([P, SLOTS], F32, name="kb_dealt")
         nc.scalar.copy(
             kb_dealt[:].rearrange("p (t c i) -> p t c i", t=PACK, i=RUN),
             kb_slots[:].rearrange("p (c t i) -> p t c i", t=PACK, i=RUN),
         )
-        kb_turned = ps.tile([P, PACK, P], F32, name="kb_turned", tag="first_bank")
+        kb_turned = ps.tile([P, PACK, P], F32, name="kb_turned")
         for t in range(PACK):
             nc.tensor.transpose(kb_turned[:, t, :], kb_dealt[:, t * P : (t + 1) * P], ident[:])
+        kb_col = sb.tile([P, PACK], F32, name="kb_col")
+        nc.scalar.copy(kb_col[:], kb_turned[:, :, ROW])
 
-        nc.vector.tensor_copy(
-            staged[:, 0:SLOTS].bitcast(I32).rearrange("p (t c) -> p t c", t=PACK),
-            ks_slots[:].bitcast(I32).rearrange("p (c t) -> p t c", t=PACK),
-        )
-        for r in range(4):
-            nc.sync.dma_start(planes[r:P:32, :].bitcast(I32), staged[STAGE + r : STAGE + 16 : 4, :].bitcast(I32))
+        q_plane = slice(SLOTS // 4, SLOTS // 4 + QW)
+        q_spare = slice(SLOTS // 4 + QW, SLOTS // 4 + 2 * QW)
+        q_both = slice(SLOTS // 4, SLOTS // 4 + 2 * QW)
+        for half in range(2):
+            nc.vector.tensor_copy(
+                plane_words[32 * half : 32 * half + 4, q_both].rearrange("p (a n) -> p a n", a=2), qs_rows[:, half::2, :]
+            )
+        nc.vector.memset(vs_pool[0:ROW, :].bitcast(I32), 0)
+        nc.vector.tensor_copy(plane_words[64:P, q_plane], plane_words[0:64, q_spare])
 
         k_codes = sb.tile([P, SLOTS], U32, name="k_codes", align_bytes=64)
         nc.vector.tensor_copy(dealt(k_codes[:]), k_pool[:].bitcast(U32).indirect(offsets[:]))
 
-        kb_col = sb.tile([P, PACK], F32, name="kb_col")
-        nc.scalar.copy(kb_col[:], kb_turned[:, :, ROW])
+        p = sb.tile([P, PACK, P], F32, name="p", tag="p_then_v_codes", align_bytes=64)
+        for t in range(PACK):
+            cols = slice(t * P, (t + 1) * P)
+            scores = ps.tile([P, P], F32, name="scores%d" % t)
+            nc.tensor.matmul_mx(
+                out=scores[:],
+                lhsT=k_codes[:, cols].bitcast(FP8X4),
+                lhsT_scale=planes[:, cols],
+                rhs=q_codes[:].bitcast(FP8X4),
+                rhs_scale=planes[:, SLOTS : SLOTS + P],
+                start=True,
+                stop=True,
+            )
+            nc.scalar.activation(p[:, t, :], scores[:], SIGMOID, bias=kb_col[:, t : t + 1])
 
         vs_slots = sb.tile([P, SLOTS], F32, name="vs_slots")
         nc.vector.tensor_copy(dealt(vs_slots[:].bitcast(U32)), vs_pool[:].bitcast(U32).indirect(offsets[:]))
@@ -104,33 +125,18 @@ def tile_attend_sigm_kb_gate_srtq128n512t2048_kernel(
         for t in range(PACK):
             nc.tensor.transpose(vs_turned[:, t, :], vs_slots[:, t * P : (t + 1) * P], ident[:])
 
-        p = sb.tile([P, PACK, P], F32, name="p", tag="p_then_v_codes", align_bytes=64)
-        for t in range(PACK):
-            cols = slice(t * P, (t + 1) * P)
-            scores = ps.tile([P, P], F32, name="scores%d" % t, tag="scores%d" % t if t else "first_bank")
-            nc.tensor.matmul_mx(
-                out=scores[:],
-                lhsT=k_codes[:, cols].bitcast(FP8X4),
-                lhsT_scale=planes[:, cols],
-                rhs=q_codes[:].bitcast(FP8X4),
-                rhs_scale=planes[:, SLOTS:],
-                start=True,
-                stop=True,
-            )
-            nc.scalar.activation(p[:, t, :], scores[:], SIGMOID, bias=kb_col[:, t : t + 1])
-
         v_slots = sb.tile([P, SLOTS], BF16, name="v_slots")
         nc.vector.tensor_copy(
             v_slots[:].rearrange("p (u c i j) -> p c u j i", u=2, i=RUN, j=2), v_pool[:].indirect(offsets[:])
         )
         v_pairs = v_slots[:].bitcast(F32)
-        v_turned = ps.tile([P, 2, P], F32, name="v_turned", tag="first_bank")
+        v_turned = ps.tile([P, 2, P], F32, name="v_turned")
         for u in range(2):
             nc.tensor.transpose(v_turned[:, u, :], v_pairs[:, u * P : (u + 1) * P], ident[:])
         v_words = sb.tile([P, P, PACK], BF16, name="v_words", align_bytes=64)
         nc.scalar.copy(v_words[:].bitcast(F32), v_turned[:].rearrange("p u e -> p e u"))
 
-        w_words = sb.tile([P, P, PACK], BF16, name="w_words", align_bytes=64)
+        w_words = reused.tile([P, P, PACK], BF16, name="w_words", align_bytes=64, offset=4096)
         for t in range(PACK):
             nc.vector.tensor_scalar_mul(w_words[:, :, t], p[:, t, :], vs_turned[:, t, ROW : ROW + 1])
         w_codes = sb.tile([P, P], U32, name="w_codes", align_bytes=64)

@@ -11,6 +11,7 @@ RUN = 4
 ROW = P - 1
 STAGE = P - 16
 QW = P // 4
+HEAD = 768
 FLOPS = 2 * 128 * 512 * 512 + 2 * 128 * 512 * 128
 BYTES = 128 * 128 * 4 + 16 * 128 + 128 * 2048 * 4 + 16 * 2048 + 128 * 2048 * 4 + 2 * 2048 * 4 + 2 * 128 * 128 * 4 + 128 * 32 * 2
 
@@ -40,12 +41,13 @@ def tile_attend_sigm_kb_gate_srtq128n512t2048_kernel(
         ps = ctx.enter_context(tc.psum_pool(name="ps", bufs=1))
 
         offsets = sb.tile([P, SLOTS // 16], U16, name="offsets")
-        ks_pool = reused.tile([P, TOKENS], U8, name="ks_pool", offset=1024)
-        gate_in = reused.tile([P, P], F32, name="gate_in", offset=0)
+        ks_pool = reused.tile([P, TOKENS], U8, name="ks_pool", offset=0)
+        gate_in = sb.tile([P, P], F32, name="gate_in", tag="gate_in_then_kb_slots")
         kb_pool = sb.tile([P, TOKENS], F32, name="kb_pool")
         vs_pool = sb.tile([P, TOKENS], F32, name="vs_pool")
         qs_rows = sb.tile([4, 4, QW], I32, name="qs_rows")
-        planes = sb.tile([P, SLOTS + 2 * P], U8, name="planes", align_bytes=64)
+        moved = sb.tile([P, SLOTS // 4], I32, name="moved")
+        q_planes = sb.tile([P, 2 * P], U8, name="q_planes", align_bytes=64)
         k_pool = sb.tile([P, TOKENS], I32, name="k_pool")
         q_codes = sb.tile([P, P], I32, name="q_codes", align_bytes=64)
         ident = sb.tile([P, P], F32, name="ident")
@@ -59,26 +61,26 @@ def tile_attend_sigm_kb_gate_srtq128n512t2048_kernel(
         nc.sync.dma_start(k_pool[:], k_words[0].rearrange("p n t -> p (n t)").bitcast(I32))
         nc.sync.dma_start(vs_pool[ROW : ROW + 1, :], vs[0:1, :])
 
-        plane_words = planes[:].bitcast(I32)
+        q_plane_words = q_planes[:].bitcast(I32)
         nc.vector.memset(ks_pool[0:STAGE, :].bitcast(I32), 0)
-        nc.vector.memset(plane_words, 0)
+        nc.vector.memset(moved[:], 0)
         nc.vector.memset(kb_pool[0:ROW, :].bitcast(I32), 0)
         nc.vector.memset(ident[:], 0.0)
         make_identity(nc, ident[:], nomemset=True)
 
         ks_slots = sb.tile([P, SLOTS], U8, name="ks_slots")
-        nc.vector.tensor_copy(dealt(ks_slots[:]), ks_pool[:].indirect(offsets[:]))
+        nc.vector.tensor_copy(ks_slots[:], ks_pool[:].indirect(offsets[:]))
 
         gate = sb.tile([P, P], F32, name="gate")
         nc.scalar.activation(gate[:], gate_in[:], SIGMOID)
 
+        v_pool = reused.tile([P, TOKENS], F32, name="v_pool", offset=0)
+        nc.sync.dma_start(v_pool[:, 0:HEAD], vT[:, 0:HEAD])
         for r in range(4):
-            queue = nc.sync if r % 2 == 0 else nc.scalar
-            queue.dma_start(plane_words[r:P:32, 0 : SLOTS // 4], ks_slots[STAGE + r : P : 4, :].bitcast(I32))
-        v_pool = reused.tile([P, TOKENS], F32, name="v_pool", offset=2048)
-        nc.sync.dma_start(v_pool[:], vT)
+            nc.sync.dma_start(moved[r:P:32, :], ks_slots[STAGE + r : P : 4, :].bitcast(I32))
+        nc.sync.dma_start(v_pool[:, HEAD:], vT[:, HEAD:])
 
-        kb_slots = reused.tile([P, SLOTS], F32, name="kb_slots", offset=0)
+        kb_slots = sb.tile([P, SLOTS], F32, name="kb_slots", tag="gate_in_then_kb_slots")
         nc.scalar.activation(kb_slots[:], kb_pool[:].indirect(offsets[:]), COPY)
         kb_dealt = sb.tile([P, SLOTS], F32, name="kb_dealt")
         nc.scalar.copy(
@@ -91,39 +93,47 @@ def tile_attend_sigm_kb_gate_srtq128n512t2048_kernel(
         kb_col = sb.tile([P, PACK], F32, name="kb_col")
         nc.scalar.copy(kb_col[:], kb_turned[:, :, ROW])
 
-        q_plane = slice(SLOTS // 4, SLOTS // 4 + QW)
-        q_spare = slice(SLOTS // 4 + QW, SLOTS // 4 + 2 * QW)
-        q_both = slice(SLOTS // 4, SLOTS // 4 + 2 * QW)
+        nc.vector.memset(q_plane_words, 0)
+        nc.vector.memset(vs_pool[0:ROW, :].bitcast(I32), 0)
         for half in range(2):
             nc.vector.tensor_copy(
-                plane_words[32 * half : 32 * half + 4, q_both].rearrange("p (a n) -> p a n", a=2), qs_rows[:, half::2, :]
+                q_plane_words[32 * half : 32 * half + 4, :].rearrange("p (a n) -> p a n", a=2), qs_rows[:, half::2, :]
             )
-        nc.vector.memset(vs_pool[0:ROW, :].bitcast(I32), 0)
-        nc.vector.tensor_copy(plane_words[64:P, q_plane], plane_words[0:64, q_spare])
+        nc.vector.tensor_copy(q_plane_words[64:P, 0:QW], q_plane_words[0:64, QW:])
+
+        vs_slots = sb.tile([P, SLOTS], F32, name="vs_slots")
+        nc.scalar.activation(vs_slots[:], vs_pool[:].indirect(offsets[:]), COPY)
+        vs_dealt = sb.tile([P, SLOTS], F32, name="vs_dealt")
+        nc.scalar.copy(
+            vs_dealt[:].rearrange("p (t c i) -> p t c i", t=PACK, i=RUN),
+            vs_slots[:].rearrange("p (c t i) -> p t c i", t=PACK, i=RUN),
+        )
 
         k_codes = sb.tile([P, SLOTS], U32, name="k_codes", align_bytes=64)
         nc.vector.tensor_copy(dealt(k_codes[:]), k_pool[:].bitcast(U32).indirect(offsets[:]))
+        k_plane = sb.tile([P, SLOTS], U8, name="k_plane", align_bytes=64)
+        nc.vector.tensor_copy(
+            k_plane[:].bitcast(I32).rearrange("p (t c) -> p t c", t=PACK), moved[:].rearrange("p (c t) -> p t c", t=PACK)
+        )
 
         p = sb.tile([P, PACK, P], F32, name="p", tag="p_then_v_codes", align_bytes=64)
         for t in range(PACK):
             cols = slice(t * P, (t + 1) * P)
-            scores = ps.tile([P, P], F32, name="scores%d" % t)
+            scores = ps.tile([P, P], F32, name="scores%d" % t, tag="scores%d" % t)
             nc.tensor.matmul_mx(
                 out=scores[:],
                 lhsT=k_codes[:, cols].bitcast(FP8X4),
-                lhsT_scale=planes[:, cols],
+                lhsT_scale=k_plane[:, cols],
                 rhs=q_codes[:].bitcast(FP8X4),
-                rhs_scale=planes[:, SLOTS : SLOTS + P],
+                rhs_scale=q_planes[:, 0:P],
                 start=True,
                 stop=True,
             )
             nc.scalar.activation(p[:, t, :], scores[:], SIGMOID, bias=kb_col[:, t : t + 1])
 
-        vs_slots = sb.tile([P, SLOTS], F32, name="vs_slots")
-        nc.vector.tensor_copy(dealt(vs_slots[:].bitcast(U32)), vs_pool[:].bitcast(U32).indirect(offsets[:]))
-        vs_turned = ps.tile([P, PACK, P], F32, name="vs_turned")
+        vs_turned = ps.tile([P, PACK, P], F32, name="vs_turned", tag="scores0")
         for t in range(PACK):
-            nc.tensor.transpose(vs_turned[:, t, :], vs_slots[:, t * P : (t + 1) * P], ident[:])
+            nc.tensor.transpose(vs_turned[:, t, :], vs_dealt[:, t * P : (t + 1) * P], ident[:])
 
         v_slots = sb.tile([P, SLOTS], BF16, name="v_slots")
         nc.vector.tensor_copy(
@@ -137,8 +147,12 @@ def tile_attend_sigm_kb_gate_srtq128n512t2048_kernel(
         nc.scalar.copy(v_words[:].bitcast(F32), v_turned[:].rearrange("p u e -> p e u"))
 
         w_words = reused.tile([P, P, PACK], BF16, name="w_words", align_bytes=64, offset=4096)
-        for t in range(PACK):
-            nc.vector.tensor_scalar_mul(w_words[:, :, t], p[:, t, :], vs_turned[:, t, ROW : ROW + 1])
+        nc.vector.tensor_tensor(
+            w_words[:].rearrange("p (c i) t -> p c t i", i=2),
+            p[:].rearrange("p t (c i) -> p c t i", i=2),
+            vs_turned[:, :, ROW : ROW + 1].to_broadcast([P, PACK, P]).rearrange("p t (c i) -> p c t i", i=2),
+            MULT,
+        )
         w_codes = sb.tile([P, P], U32, name="w_codes", align_bytes=64)
         w_plane = sb.tile([P, P], U8, name="w_plane", align_bytes=64)
         nc.vector.quantize_mx(w_codes[:].bitcast(FP8X4), w_plane[:], w_words[:].rearrange("p q t -> p (q t)"))

@@ -56,10 +56,10 @@ def tile_attend_sigm_kb_gate_srtq128n512t2048_kernel(
         nc.sync.dma_start(offsets[:], offs)
         nc.scalar.dma_start(gate_in[:], og[0])
         nc.sync.dma_start(kb_pool[ROW : ROW + 1, :], kb[0:1, :])
-        nc.sync.dma_start(qs_rows[:], q_scales[0, 0].bitcast(I32).rearrange("(a j) n -> j a n", j=4))
         nc.scalar.dma_start(q_codes[:], q_words[0, 0].rearrange("p n t -> p (n t)").bitcast(I32))
-        nc.sync.dma_start(k_pool[:], k_words[0].rearrange("p n t -> p (n t)").bitcast(I32))
+        nc.sync.dma_start(qs_rows[:], q_scales[0, 0].bitcast(I32).rearrange("(a j) n -> j a n", j=4))
         nc.sync.dma_start(vs_pool[ROW : ROW + 1, :], vs[0:1, :])
+        nc.sync.dma_start(k_pool[:], k_words[0].rearrange("p n t -> p (n t)").bitcast(I32))
 
         q_plane_words = q_planes[:].bitcast(I32)
         nc.vector.memset(ks_pool[0:STAGE, :].bitcast(I32), 0)

@@ -7,11 +7,14 @@ P = 128
 TOKENS = 2048
 SLOTS = 512
 PACK = 4
-RUN = 4
+RUN = 2
 ROW = P - 1
 STAGE = P - 16
 QW = P // 4
 HEAD = 768
+EARLY = 384
+HALF = SLOTS // 2
+PREFIX = TOKENS - HALF
 FLOPS = 2 * 128 * 512 * 512 + 2 * 128 * 512 * 128
 BYTES = 128 * 128 * 4 + 16 * 128 + 128 * 2048 * 4 + 16 * 2048 + 128 * 2048 * 4 + 2 * 2048 * 4 + 2 * 128 * 128 * 4 + 128 * 32 * 2
 
@@ -55,9 +58,9 @@ def tile_attend_sigm_kb_gate_srtq128n512t2048_kernel(
         nc.scalar.dma_start(ks_pool[STAGE:, :].bitcast(I32), k_scales[0].bitcast(I32))
         nc.sync.dma_start(offsets[:], offs)
         nc.scalar.dma_start(gate_in[:], og[0])
-        nc.sync.dma_start(kb_pool[ROW : ROW + 1, :], kb[0:1, :])
-        nc.scalar.dma_start(q_codes[:], q_words[0, 0].rearrange("p n t -> p (n t)").bitcast(I32))
         nc.sync.dma_start(qs_rows[:], q_scales[0, 0].bitcast(I32).rearrange("(a j) n -> j a n", j=4))
+        nc.scalar.dma_start(q_codes[:], q_words[0, 0].rearrange("p n t -> p (n t)").bitcast(I32))
+        nc.sync.dma_start(kb_pool[ROW : ROW + 1, :], kb[0:1, :])
         nc.sync.dma_start(vs_pool[ROW : ROW + 1, :], vs[0:1, :])
         nc.sync.dma_start(k_pool[:], k_words[0].rearrange("p n t -> p (n t)").bitcast(I32))
 
@@ -65,6 +68,7 @@ def tile_attend_sigm_kb_gate_srtq128n512t2048_kernel(
         nc.vector.memset(ks_pool[0:STAGE, :].bitcast(I32), 0)
         nc.vector.memset(moved[:], 0)
         nc.vector.memset(kb_pool[0:ROW, :].bitcast(I32), 0)
+        nc.vector.memset(vs_pool[0:ROW, 0:EARLY].bitcast(I32), 0)
         nc.vector.memset(ident[:], 0.0)
         make_identity(nc, ident[:], nomemset=True)
 
@@ -78,7 +82,8 @@ def tile_attend_sigm_kb_gate_srtq128n512t2048_kernel(
         nc.sync.dma_start(v_pool[:, 0:HEAD], vT[:, 0:HEAD])
         for r in range(4):
             nc.sync.dma_start(moved[r:P:32, :], ks_slots[STAGE + r : P : 4, :].bitcast(I32))
-        nc.sync.dma_start(v_pool[:, HEAD:], vT[:, HEAD:])
+        nc.sync.dma_start(v_pool[:, HEAD:PREFIX], vT[:, HEAD:PREFIX])
+        nc.sync.dma_start(v_pool[:, PREFIX:], vT[:, PREFIX:])
 
         kb_slots = sb.tile([P, SLOTS], F32, name="kb_slots", tag="gate_in_then_kb_slots")
         nc.scalar.activation(kb_slots[:], kb_pool[:].indirect(offsets[:]), COPY)
@@ -94,7 +99,7 @@ def tile_attend_sigm_kb_gate_srtq128n512t2048_kernel(
         nc.scalar.copy(kb_col[:], kb_turned[:, :, ROW])
 
         nc.vector.memset(q_plane_words, 0)
-        nc.vector.memset(vs_pool[0:ROW, :].bitcast(I32), 0)
+        nc.vector.memset(vs_pool[0:ROW, EARLY:].bitcast(I32), 0)
         for half in range(2):
             nc.vector.tensor_copy(
                 q_plane_words[32 * half : 32 * half + 4, :].rearrange("p (a n) -> p a n", a=2), qs_rows[:, half::2, :]
@@ -113,7 +118,8 @@ def tile_attend_sigm_kb_gate_srtq128n512t2048_kernel(
         nc.vector.tensor_copy(dealt(k_codes[:]), k_pool[:].bitcast(U32).indirect(offsets[:]))
         k_plane = sb.tile([P, SLOTS], U8, name="k_plane", align_bytes=64)
         nc.vector.tensor_copy(
-            k_plane[:].bitcast(I32).rearrange("p (t c) -> p t c", t=PACK), moved[:].rearrange("p (c t) -> p t c", t=PACK)
+            k_plane[:].bitcast(U16).rearrange("p (t c) -> p t c", t=PACK),
+            moved[:].bitcast(U16).rearrange("p (c t) -> p t c", t=PACK),
         )
 
         p = sb.tile([P, PACK, P], F32, name="p", tag="p_then_v_codes", align_bytes=64)
@@ -131,18 +137,20 @@ def tile_attend_sigm_kb_gate_srtq128n512t2048_kernel(
             )
             nc.scalar.activation(p[:, t, :], scores[:], SIGMOID, bias=kb_col[:, t : t + 1])
 
-        vs_turned = ps.tile([P, PACK, P], F32, name="vs_turned", tag="scores0")
+        vs_turned = ps.tile([P, PACK, P], F32, name="vs_turned")
         for t in range(PACK):
             nc.tensor.transpose(vs_turned[:, t, :], vs_dealt[:, t * P : (t + 1) * P], ident[:])
 
         v_slots = sb.tile([P, SLOTS], BF16, name="v_slots")
-        nc.vector.tensor_copy(
-            v_slots[:].rearrange("p (u c i j) -> p c u j i", u=2, i=RUN, j=2), v_pool[:].indirect(offsets[:])
-        )
+        for half, window in enumerate((v_pool[:, 0:PREFIX], v_pool[:])):
+            nc.vector.tensor_copy(
+                v_slots[:, half * HALF : (half + 1) * HALF].rearrange("p (c i t) -> p c t i", i=RUN, t=PACK),
+                window.indirect(offsets[:, half * HALF // 16 : (half + 1) * HALF // 16]),
+            )
         v_pairs = v_slots[:].bitcast(F32)
         v_turned = ps.tile([P, 2, P], F32, name="v_turned")
         for u in range(2):
-            nc.tensor.transpose(v_turned[:, u, :], v_pairs[:, u * P : (u + 1) * P], ident[:])
+            nc.tensor.transpose(v_turned[:, u, :], v_pairs[:, u::2], ident[:])
         v_words = sb.tile([P, P, PACK], BF16, name="v_words", align_bytes=64)
         nc.scalar.copy(v_words[:].bitcast(F32), v_turned[:].rearrange("p u e -> p e u"))
 

@@ -12,7 +12,7 @@ ROW = P - 1
 STAGE = P - 16
 QW = P // 4
 HEAD = 768
-EARLY = 384
+EARLY = 256
 HALF = SLOTS // 2
 PREFIX = TOKENS - HALF
 FLOPS = 2 * 128 * 512 * 512 + 2 * 128 * 512 * 128
@@ -106,14 +106,6 @@ def tile_attend_sigm_kb_gate_srtq128n512t2048_kernel(
             )
         nc.vector.tensor_copy(q_plane_words[64:P, 0:QW], q_plane_words[0:64, QW:])
 
-        vs_slots = sb.tile([P, SLOTS], F32, name="vs_slots")
-        nc.scalar.activation(vs_slots[:], vs_pool[:].indirect(offsets[:]), COPY)
-        vs_dealt = sb.tile([P, SLOTS], F32, name="vs_dealt")
-        nc.scalar.copy(
-            vs_dealt[:].rearrange("p (t c i) -> p t c i", t=PACK, i=RUN),
-            vs_slots[:].rearrange("p (c t i) -> p t c i", t=PACK, i=RUN),
-        )
-
         k_codes = sb.tile([P, SLOTS], U32, name="k_codes", align_bytes=64)
         nc.vector.tensor_copy(dealt(k_codes[:]), k_pool[:].bitcast(U32).indirect(offsets[:]))
         k_plane = sb.tile([P, SLOTS], U8, name="k_plane", align_bytes=64)
@@ -137,6 +129,8 @@ def tile_attend_sigm_kb_gate_srtq128n512t2048_kernel(
             )
             nc.scalar.activation(p[:, t, :], scores[:], SIGMOID, bias=kb_col[:, t : t + 1])
 
+        vs_dealt = sb.tile([P, SLOTS], F32, name="vs_dealt")
+        nc.vector.tensor_copy(dealt(vs_dealt[:].bitcast(U32)), vs_pool[:].bitcast(U32).indirect(offsets[:]))
         vs_turned = ps.tile([P, PACK, P], F32, name="vs_turned")
         for t in range(PACK):
             nc.tensor.transpose(vs_turned[:, t, :], vs_dealt[:, t * P : (t + 1) * P], ident[:])

@@ -7,12 +7,14 @@ P = 128
 TOKENS = 2048
 SLOTS = 512
 PACK = 4
-RUN = 2
+RUN = 4
 ROW = P - 1
 STAGE = P - 16
+KW = SLOTS // 4
 QW = P // 4
-HEAD = 768
-EARLY = 256
+HEAD = 1152
+EARLY = 512
+WAIT = 512
 HALF = SLOTS // 2
 PREFIX = TOKENS - HALF
 FLOPS = 2 * 128 * 512 * 512 + 2 * 128 * 512 * 128
@@ -48,9 +50,8 @@ def tile_attend_sigm_kb_gate_srtq128n512t2048_kernel(
         gate_in = sb.tile([P, P], F32, name="gate_in", tag="gate_in_then_kb_slots")
         kb_pool = sb.tile([P, TOKENS], F32, name="kb_pool")
         vs_pool = sb.tile([P, TOKENS], F32, name="vs_pool")
-        qs_rows = sb.tile([4, 4, QW], I32, name="qs_rows")
-        moved = sb.tile([P, SLOTS // 4], I32, name="moved")
-        q_planes = sb.tile([P, 2 * P], U8, name="q_planes", align_bytes=64)
+        staged = sb.tile([P, KW + QW], I32, name="staged")
+        planes = sb.tile([P, SLOTS + P], U8, name="planes", align_bytes=64)
         k_pool = sb.tile([P, TOKENS], I32, name="k_pool")
         q_codes = sb.tile([P, P], I32, name="q_codes", align_bytes=64)
         ident = sb.tile([P, P], F32, name="ident")
@@ -58,22 +59,27 @@ def tile_attend_sigm_kb_gate_srtq128n512t2048_kernel(
         nc.scalar.dma_start(ks_pool[STAGE:, :].bitcast(I32), k_scales[0].bitcast(I32))
         nc.sync.dma_start(offsets[:], offs)
         nc.scalar.dma_start(gate_in[:], og[0])
-        nc.sync.dma_start(qs_rows[:], q_scales[0, 0].bitcast(I32).rearrange("(a j) n -> j a n", j=4))
+        nc.sync.dma_start(staged[STAGE:, KW:], q_scales[0, 0].bitcast(I32))
         nc.scalar.dma_start(q_codes[:], q_words[0, 0].rearrange("p n t -> p (n t)").bitcast(I32))
         nc.sync.dma_start(kb_pool[ROW : ROW + 1, :], kb[0:1, :])
         nc.sync.dma_start(vs_pool[ROW : ROW + 1, :], vs[0:1, :])
         nc.sync.dma_start(k_pool[:], k_words[0].rearrange("p n t -> p (n t)").bitcast(I32))
 
-        q_plane_words = q_planes[:].bitcast(I32)
+        plane_words = planes[:].bitcast(I32)
         nc.vector.memset(ks_pool[0:STAGE, :].bitcast(I32), 0)
-        nc.vector.memset(moved[:], 0)
         nc.vector.memset(kb_pool[0:ROW, :].bitcast(I32), 0)
-        nc.vector.memset(vs_pool[0:ROW, 0:EARLY].bitcast(I32), 0)
+        nc.vector.memset(plane_words, 0)
         nc.vector.memset(ident[:], 0.0)
+        nc.vector.memset(vs_pool[0:ROW, 0:EARLY].bitcast(I32), 0)
         make_identity(nc, ident[:], nomemset=True)
 
         ks_slots = sb.tile([P, SLOTS], U8, name="ks_slots")
         nc.vector.tensor_copy(ks_slots[:], ks_pool[:].indirect(offsets[:]))
+        nc.vector.memset(vs_pool[0:ROW, EARLY : EARLY + WAIT].bitcast(I32), 0)
+        nc.vector.tensor_copy(
+            staged[:, 0:KW].rearrange("p (t c) -> p t c", t=PACK),
+            ks_slots[:].bitcast(I32).rearrange("p (c t) -> p t c", t=PACK),
+        )
 
         gate = sb.tile([P, P], F32, name="gate")
         nc.scalar.activation(gate[:], gate_in[:], SIGMOID)
@@ -81,7 +87,7 @@ def tile_attend_sigm_kb_gate_srtq128n512t2048_kernel(
         v_pool = reused.tile([P, TOKENS], F32, name="v_pool", offset=0)
         nc.sync.dma_start(v_pool[:, 0:HEAD], vT[:, 0:HEAD])
         for r in range(4):
-            nc.sync.dma_start(moved[r:P:32, :], ks_slots[STAGE + r : P : 4, :].bitcast(I32))
+            nc.sync.dma_start(plane_words[r:P:32, :], staged[STAGE + r : P : 4, :])
         nc.sync.dma_start(v_pool[:, HEAD:PREFIX], vT[:, HEAD:PREFIX])
         nc.sync.dma_start(v_pool[:, PREFIX:], vT[:, PREFIX:])
 
@@ -98,21 +104,10 @@ def tile_attend_sigm_kb_gate_srtq128n512t2048_kernel(
         kb_col = sb.tile([P, PACK], F32, name="kb_col")
         nc.scalar.copy(kb_col[:], kb_turned[:, :, ROW])
 
-        nc.vector.memset(q_plane_words, 0)
-        nc.vector.memset(vs_pool[0:ROW, EARLY:].bitcast(I32), 0)
-        for half in range(2):
-            nc.vector.tensor_copy(
-                q_plane_words[32 * half : 32 * half + 4, :].rearrange("p (a n) -> p a n", a=2), qs_rows[:, half::2, :]
-            )
-        nc.vector.tensor_copy(q_plane_words[64:P, 0:QW], q_plane_words[0:64, QW:])
+        nc.vector.memset(vs_pool[0:ROW, EARLY + WAIT :].bitcast(I32), 0)
 
         k_codes = sb.tile([P, SLOTS], U32, name="k_codes", align_bytes=64)
         nc.vector.tensor_copy(dealt(k_codes[:]), k_pool[:].bitcast(U32).indirect(offsets[:]))
-        k_plane = sb.tile([P, SLOTS], U8, name="k_plane", align_bytes=64)
-        nc.vector.tensor_copy(
-            k_plane[:].bitcast(U16).rearrange("p (t c) -> p t c", t=PACK),
-            moved[:].bitcast(U16).rearrange("p (c t) -> p t c", t=PACK),
-        )
 
         p = sb.tile([P, PACK, P], F32, name="p", tag="p_then_v_codes", align_bytes=64)
         for t in range(PACK):
@@ -121,9 +116,9 @@ def tile_attend_sigm_kb_gate_srtq128n512t2048_kernel(
             nc.tensor.matmul_mx(
                 out=scores[:],
                 lhsT=k_codes[:, cols].bitcast(FP8X4),
-                lhsT_scale=k_plane[:, cols],
+                lhsT_scale=planes[:, cols],
                 rhs=q_codes[:].bitcast(FP8X4),
-                rhs_scale=q_planes[:, 0:P],
+                rhs_scale=planes[:, SLOTS:],
                 start=True,
                 stop=True,
             )
@@ -136,15 +131,14 @@ def tile_attend_sigm_kb_gate_srtq128n512t2048_kernel(
             nc.tensor.transpose(vs_turned[:, t, :], vs_dealt[:, t * P : (t + 1) * P], ident[:])
 
         v_slots = sb.tile([P, SLOTS], BF16, name="v_slots")
+        v_dealt = v_slots[:].rearrange("p (u c i h) -> p c u h i", u=2, i=RUN, h=2)
         for half, window in enumerate((v_pool[:, 0:PREFIX], v_pool[:])):
-            nc.vector.tensor_copy(
-                v_slots[:, half * HALF : (half + 1) * HALF].rearrange("p (c i t) -> p c t i", i=RUN, t=PACK),
-                window.indirect(offsets[:, half * HALF // 16 : (half + 1) * HALF // 16]),
-            )
+            cols = slice(half * HALF // 16, (half + 1) * HALF // 16)
+            nc.vector.tensor_copy(v_dealt[:, cols], window.indirect(offsets[:, cols]))
         v_pairs = v_slots[:].bitcast(F32)
         v_turned = ps.tile([P, 2, P], F32, name="v_turned")
         for u in range(2):
-            nc.tensor.transpose(v_turned[:, u, :], v_pairs[:, u::2], ident[:])
+            nc.tensor.transpose(v_turned[:, u, :], v_pairs[:, u * P : (u + 1) * P], ident[:])
         v_words = sb.tile([P, P, PACK], BF16, name="v_words", align_bytes=64)
         nc.scalar.copy(v_words[:].bitcast(F32), v_turned[:].rearrange("p u e -> p e u"))
 

@@ -9,12 +9,11 @@ SLOTS = 512
 PACK = 4
 RUN = 4
 ROW = P - 1
-STAGE = P - 16
+STAGE = 48
 KW = SLOTS // 4
 QW = P // 4
 HEAD = 1152
-EARLY = 512
-WAIT = 512
+WAIT = 384
 HALF = SLOTS // 2
 PREFIX = TOKENS - HALF
 FLOPS = 2 * 128 * 512 * 512 + 2 * 128 * 512 * 128
@@ -56,26 +55,26 @@ def tile_attend_sigm_kb_gate_srtq128n512t2048_kernel(
         q_codes = sb.tile([P, P], I32, name="q_codes", align_bytes=64)
         ident = sb.tile([P, P], F32, name="ident")
 
-        nc.scalar.dma_start(ks_pool[STAGE:, :].bitcast(I32), k_scales[0].bitcast(I32))
+        nc.scalar.dma_start(ks_pool[STAGE : STAGE + 16, :].bitcast(I32), k_scales[0].bitcast(I32))
         nc.sync.dma_start(offsets[:], offs)
         nc.scalar.dma_start(gate_in[:], og[0])
-        nc.sync.dma_start(staged[STAGE:, KW:], q_scales[0, 0].bitcast(I32))
         nc.scalar.dma_start(q_codes[:], q_words[0, 0].rearrange("p n t -> p (n t)").bitcast(I32))
         nc.sync.dma_start(kb_pool[ROW : ROW + 1, :], kb[0:1, :])
         nc.sync.dma_start(vs_pool[ROW : ROW + 1, :], vs[0:1, :])
+        nc.sync.dma_start(staged[STAGE : STAGE + 16, KW:], q_scales[0, 0].bitcast(I32))
         nc.sync.dma_start(k_pool[:], k_words[0].rearrange("p n t -> p (n t)").bitcast(I32))
 
         plane_words = planes[:].bitcast(I32)
+        nc.vector.memset(ks_pool[STAGE + 16 :, :].bitcast(I32), 0)
         nc.vector.memset(ks_pool[0:STAGE, :].bitcast(I32), 0)
         nc.vector.memset(kb_pool[0:ROW, :].bitcast(I32), 0)
-        nc.vector.memset(plane_words, 0)
         nc.vector.memset(ident[:], 0.0)
-        nc.vector.memset(vs_pool[0:ROW, 0:EARLY].bitcast(I32), 0)
         make_identity(nc, ident[:], nomemset=True)
 
         ks_slots = sb.tile([P, SLOTS], U8, name="ks_slots")
         nc.vector.tensor_copy(ks_slots[:], ks_pool[:].indirect(offsets[:]))
-        nc.vector.memset(vs_pool[0:ROW, EARLY : EARLY + WAIT].bitcast(I32), 0)
+        nc.vector.memset(plane_words, 0)
+        nc.vector.memset(vs_pool[0:ROW, 0:WAIT].bitcast(I32), 0)
         nc.vector.tensor_copy(
             staged[:, 0:KW].rearrange("p (t c) -> p t c", t=PACK),
             ks_slots[:].bitcast(I32).rearrange("p (c t) -> p t c", t=PACK),
@@ -87,7 +86,7 @@ def tile_attend_sigm_kb_gate_srtq128n512t2048_kernel(
         v_pool = reused.tile([P, TOKENS], F32, name="v_pool", offset=0)
         nc.sync.dma_start(v_pool[:, 0:HEAD], vT[:, 0:HEAD])
         for r in range(4):
-            nc.sync.dma_start(plane_words[r:P:32, :], staged[STAGE + r : P : 4, :])
+            nc.sync.dma_start(plane_words[r:P:32, :], staged[STAGE + r : STAGE + 16 : 4, :])
         nc.sync.dma_start(v_pool[:, HEAD:PREFIX], vT[:, HEAD:PREFIX])
         nc.sync.dma_start(v_pool[:, PREFIX:], vT[:, PREFIX:])
 
@@ -104,7 +103,7 @@ def tile_attend_sigm_kb_gate_srtq128n512t2048_kernel(
         kb_col = sb.tile([P, PACK], F32, name="kb_col")
         nc.scalar.copy(kb_col[:], kb_turned[:, :, ROW])
 
-        nc.vector.memset(vs_pool[0:ROW, EARLY + WAIT :].bitcast(I32), 0)
+        nc.vector.memset(vs_pool[0:ROW, WAIT:].bitcast(I32), 0)
 
         k_codes = sb.tile([P, SLOTS], U32, name="k_codes", align_bytes=64)
         nc.vector.tensor_copy(dealt(k_codes[:]), k_pool[:].bitcast(U32).indirect(offsets[:]))

@@ -15,6 +15,8 @@ QW = P // 4
 HEAD = 1152
 WAIT = 384
 HALF = SLOTS // 2
+SHARE = 128
+CUT = (SLOTS - SHARE) // 16
 PREFIX = TOKENS - HALF
 FLOPS = 2 * 128 * 512 * 512 + 2 * 128 * 512 * 128
 BYTES = 128 * 128 * 4 + 16 * 128 + 128 * 2048 * 4 + 16 * 2048 + 128 * 2048 * 4 + 2 * 2048 * 4 + 2 * 128 * 128 * 4 + 128 * 32 * 2
@@ -100,10 +102,17 @@ def tile_attend_sigm_kb_gate_srtq128n512t2048_kernel(
         kb_turned = ps.tile([P, PACK, P], F32, name="kb_turned")
         for t in range(PACK):
             nc.tensor.transpose(kb_turned[:, t, :], kb_dealt[:, t * P : (t + 1) * P], ident[:])
-        kb_col = sb.tile([P, PACK], F32, name="kb_col")
-        nc.scalar.copy(kb_col[:], kb_turned[:, :, ROW])
-
         nc.vector.memset(vs_pool[0:ROW, WAIT:].bitcast(I32), 0)
+
+        vs_slots = sb.tile([P, SHARE], F32, name="vs_slots", tag="vs_slots_then_kb_col")
+        nc.scalar.activation(vs_slots[:], vs_pool[:].indirect(offsets[:, CUT:]), COPY)
+        vs_dealt = sb.tile([P, SLOTS], F32, name="vs_dealt")
+        nc.scalar.copy(
+            vs_dealt[:].rearrange("p (t c i) -> p t c i", t=PACK, i=RUN)[:, :, CUT:],
+            vs_slots[:].rearrange("p (c t i) -> p t c i", t=PACK, i=RUN),
+        )
+        kb_col = sb.tile([P, PACK], F32, name="kb_col", tag="vs_slots_then_kb_col")
+        nc.scalar.copy(kb_col[:], kb_turned[:, :, ROW])
 
         k_codes = sb.tile([P, SLOTS], U32, name="k_codes", align_bytes=64)
         nc.vector.tensor_copy(dealt(k_codes[:]), k_pool[:].bitcast(U32).indirect(offsets[:]))
@@ -123,8 +132,9 @@ def tile_attend_sigm_kb_gate_srtq128n512t2048_kernel(
             )
             nc.scalar.activation(p[:, t, :], scores[:], SIGMOID, bias=kb_col[:, t : t + 1])
 
-        vs_dealt = sb.tile([P, SLOTS], F32, name="vs_dealt")
-        nc.vector.tensor_copy(dealt(vs_dealt[:].bitcast(U32)), vs_pool[:].bitcast(U32).indirect(offsets[:]))
+        nc.vector.tensor_copy(
+            dealt(vs_dealt[:].bitcast(U32))[:, 0:CUT], vs_pool[:].bitcast(U32).indirect(offsets[:, 0:CUT])
+        )
         vs_turned = ps.tile([P, PACK, P], F32, name="vs_turned")
         for t in range(PACK):
             nc.tensor.transpose(vs_turned[:, t, :], vs_dealt[:, t * P : (t + 1) * P], ident[:])

from contextlib import ExitStack

import concourse.mybir as mybir
from concourse.masks import make_identity

P = 128
TOKENS = 2048
SLOTS = 512
PACK = 4
RUN = 4
ROW = P - 1
STAGE = 48
KW = SLOTS // 4
QW = P // 4
HEAD = 1152
WAIT = 384
HALF = SLOTS // 2
SHARE = 128
CUT = (SLOTS - SHARE) // 16
PREFIX = TOKENS - HALF
FLOPS = 2 * 128 * 512 * 512 + 2 * 128 * 512 * 128
BYTES = 128 * 128 * 4 + 16 * 128 + 128 * 2048 * 4 + 16 * 2048 + 128 * 2048 * 4 + 2 * 2048 * 4 + 2 * 128 * 128 * 4 + 128 * 32 * 2

F32 = mybir.dt.float32
BF16 = mybir.dt.bfloat16
I32 = mybir.dt.int32
U32 = mybir.dt.uint32
U16 = mybir.dt.uint16
U8 = mybir.dt.uint8
FP8X4 = mybir.dt.float8_e4m3fn_x4
MULT = mybir.AluOpType.mult
SIGMOID = mybir.ActivationFunctionType.Sigmoid
COPY = mybir.ActivationFunctionType.Copy


def dealt(words):
    return words.rearrange("p (t c i) -> p c t i", t=PACK, i=RUN)


def tile_attend_sigm_kb_gate_srtq128n512t2048_kernel(
    tc, q_words, q_scales, k_words, k_scales, vT, vs, kb, og, offs, out
):
    nc = tc.nc
    with ExitStack() as ctx:
        sb = ctx.enter_context(tc.tile_pool(name="sb", bufs=1))
        reused = ctx.enter_context(tc.tile_pool(name="reused", bufs=1))
        ps = ctx.enter_context(tc.psum_pool(name="ps", bufs=1))

        offsets = sb.tile([P, SLOTS // 16], U16, name="offsets")
        ks_pool = reused.tile([P, TOKENS], U8, name="ks_pool", offset=0)
        gate_in = sb.tile([P, P], F32, name="gate_in", tag="gate_in_then_kb_slots")
        kb_pool = sb.tile([P, TOKENS], F32, name="kb_pool")
        vs_pool = sb.tile([P, TOKENS], F32, name="vs_pool")
        staged = sb.tile([P, KW + QW], I32, name="staged")
        planes = sb.tile([P, SLOTS + P], U8, name="planes", align_bytes=64)
        k_pool = sb.tile([P, TOKENS], I32, name="k_pool")
        q_codes = sb.tile([P, P], I32, name="q_codes", align_bytes=64)
        ident = sb.tile([P, P], F32, name="ident")

        nc.scalar.dma_start(ks_pool[STAGE : STAGE + 16, :].bitcast(I32), k_scales[0].bitcast(I32))
        nc.sync.dma_start(offsets[:], offs)
        nc.scalar.dma_start(gate_in[:], og[0])
        nc.scalar.dma_start(q_codes[:], q_words[0, 0].rearrange("p n t -> p (n t)").bitcast(I32))
        nc.sync.dma_start(kb_pool[ROW : ROW + 1, :], kb[0:1, :])
        nc.sync.dma_start(vs_pool[ROW : ROW + 1, :], vs[0:1, :])
        nc.sync.dma_start(staged[STAGE : STAGE + 16, KW:], q_scales[0, 0].bitcast(I32))
        nc.sync.dma_start(k_pool[:], k_words[0].rearrange("p n t -> p (n t)").bitcast(I32))

        plane_words = planes[:].bitcast(I32)
        nc.vector.memset(ks_pool[STAGE + 16 :, :].bitcast(I32), 0)
        nc.vector.memset(ks_pool[0:STAGE, :].bitcast(I32), 0)
        nc.vector.memset(kb_pool[0:ROW, :].bitcast(I32), 0)
        nc.vector.memset(ident[:], 0.0)
        make_identity(nc, ident[:], nomemset=True)

        ks_slots = sb.tile([P, SLOTS], U8, name="ks_slots")
        nc.vector.tensor_copy(ks_slots[:], ks_pool[:].indirect(offsets[:]))
        nc.vector.memset(plane_words, 0)
        nc.vector.memset(vs_pool[0:ROW, 0:WAIT].bitcast(I32), 0)
        nc.vector.tensor_copy(
            staged[:, 0:KW].rearrange("p (t c) -> p t c", t=PACK),
            ks_slots[:].bitcast(I32).rearrange("p (c t) -> p t c", t=PACK),
        )

        gate = sb.tile([P, P], F32, name="gate")
        nc.scalar.activation(gate[:], gate_in[:], SIGMOID)

        v_pool = reused.tile([P, TOKENS], F32, name="v_pool", offset=0)
        nc.sync.dma_start(v_pool[:, 0:HEAD], vT[:, 0:HEAD])
        for r in range(4):
            nc.sync.dma_start(plane_words[r:P:32, :], staged[STAGE + r : STAGE + 16 : 4, :])
        nc.sync.dma_start(v_pool[:, HEAD:PREFIX], vT[:, HEAD:PREFIX])
        nc.sync.dma_start(v_pool[:, PREFIX:], vT[:, PREFIX:])

        kb_slots = sb.tile([P, SLOTS], F32, name="kb_slots", tag="gate_in_then_kb_slots")
        nc.scalar.activation(kb_slots[:], kb_pool[:].indirect(offsets[:]), COPY)
        kb_dealt = sb.tile([P, SLOTS], F32, name="kb_dealt")
        nc.scalar.copy(
            kb_dealt[:].rearrange("p (t c i) -> p t c i", t=PACK, i=RUN),
            kb_slots[:].rearrange("p (c t i) -> p t c i", t=PACK, i=RUN),
        )
        kb_turned = ps.tile([P, PACK, P], F32, name="kb_turned")
        for t in range(PACK):
            nc.tensor.transpose(kb_turned[:, t, :], kb_dealt[:, t * P : (t + 1) * P], ident[:])
        nc.vector.memset(vs_pool[0:ROW, WAIT:].bitcast(I32), 0)

        vs_slots = sb.tile([P, SHARE], F32, name="vs_slots", tag="vs_slots_then_kb_col")
        nc.scalar.activation(vs_slots[:], vs_pool[:].indirect(offsets[:, CUT:]), COPY)
        vs_dealt = sb.tile([P, SLOTS], F32, name="vs_dealt")
        nc.scalar.copy(
            vs_dealt[:].rearrange("p (t c i) -> p t c i", t=PACK, i=RUN)[:, :, CUT:],
            vs_slots[:].rearrange("p (c t i) -> p t c i", t=PACK, i=RUN),
        )
        kb_col = sb.tile([P, PACK], F32, name="kb_col", tag="vs_slots_then_kb_col")
        nc.scalar.copy(kb_col[:], kb_turned[:, :, ROW])

        k_codes = sb.tile([P, SLOTS], U32, name="k_codes", align_bytes=64)
        nc.vector.tensor_copy(dealt(k_codes[:]), k_pool[:].bitcast(U32).indirect(offsets[:]))

        p = sb.tile([P, PACK, P], F32, name="p", tag="p_then_v_codes", align_bytes=64)
        for t in range(PACK):
            cols = slice(t * P, (t + 1) * P)
            scores = ps.tile([P, P], F32, name="scores%d" % t, tag="scores%d" % t)
            nc.tensor.matmul_mx(
                out=scores[:],
                lhsT=k_codes[:, cols].bitcast(FP8X4),
                lhsT_scale=planes[:, cols],
                rhs=q_codes[:].bitcast(FP8X4),
                rhs_scale=planes[:, SLOTS:],
                start=True,
                stop=True,
            )
            nc.scalar.activation(p[:, t, :], scores[:], SIGMOID, bias=kb_col[:, t : t + 1])

        nc.vector.tensor_copy(
            dealt(vs_dealt[:].bitcast(U32))[:, 0:CUT], vs_pool[:].bitcast(U32).indirect(offsets[:, 0:CUT])
        )
        vs_turned = ps.tile([P, PACK, P], F32, name="vs_turned")
        for t in range(PACK):
            nc.tensor.transpose(vs_turned[:, t, :], vs_dealt[:, t * P : (t + 1) * P], ident[:])

        v_slots = sb.tile([P, SLOTS], BF16, name="v_slots")
        v_dealt = v_slots[:].rearrange("p (u c i h) -> p c u h i", u=2, i=RUN, h=2)
        for half, window in enumerate((v_pool[:, 0:PREFIX], v_pool[:])):
            cols = slice(half * HALF // 16, (half + 1) * HALF // 16)
            nc.vector.tensor_copy(v_dealt[:, cols], window.indirect(offsets[:, cols]))
        v_pairs = v_slots[:].bitcast(F32)
        v_turned = ps.tile([P, 2, P], F32, name="v_turned")
        for u in range(2):
            nc.tensor.transpose(v_turned[:, u, :], v_pairs[:, u * P : (u + 1) * P], ident[:])
        v_words = sb.tile([P, P, PACK], BF16, name="v_words", align_bytes=64)
        nc.scalar.copy(v_words[:].bitcast(F32), v_turned[:].rearrange("p u e -> p e u"))

        w_words = reused.tile([P, P, PACK], BF16, name="w_words", align_bytes=64, offset=4096)
        nc.vector.tensor_tensor(
            w_words[:].rearrange("p (c i) t -> p c t i", i=2),
            p[:].rearrange("p t (c i) -> p c t i", i=2),
            vs_turned[:, :, ROW : ROW + 1].to_broadcast([P, PACK, P]).rearrange("p t (c i) -> p c t i", i=2),
            MULT,
        )
        w_codes = sb.tile([P, P], U32, name="w_codes", align_bytes=64)
        w_plane = sb.tile([P, P], U8, name="w_plane", align_bytes=64)
        nc.vector.quantize_mx(w_codes[:].bitcast(FP8X4), w_plane[:], w_words[:].rearrange("p q t -> p (q t)"))
        v_codes = sb.tile([P, P], U32, name="v_codes", tag="p_then_v_codes", align_bytes=64)
        v_plane = sb.tile([P, P], U8, name="v_plane", align_bytes=64)
        nc.vector.quantize_mx(v_codes[:].bitcast(FP8X4), v_plane[:], v_words[:].rearrange("p e t -> p (e t)"))

        y = ps.tile([P, P], F32, name="y")
        nc.tensor.matmul_mx(
            out=y[:],
            lhsT=w_codes[:].bitcast(FP8X4),
            lhsT_scale=w_plane[:],
            rhs=v_codes[:].bitcast(FP8X4),
            rhs_scale=v_plane[:],
            start=True,
            stop=True,
        )
        result = sb.tile([P, P], F32, name="result")
        nc.vector.scalar_tensor_tensor(result[:], y[:], 1.0 / 16.0, gate[:], MULT, MULT)
        nc.sync.dma_start(out[0], result[:])
